import numpy as np
import ml_dtypes


def mxq(x, axis, fmt="e4m3"):
    dtype, down = {"e4m3": (ml_dtypes.float8_e4m3fn, 7), "e5m2": (ml_dtypes.float8_e5m2, 14)}[fmt]
    v = np.moveaxis(np.asarray(x, np.float32).astype(ml_dtypes.bfloat16).astype(np.float64), axis, -1)
    blocks = v.reshape(v.shape[:-1] + (-1, 32))
    amax = np.abs(blocks).max(-1, keepdims=True)
    byte = np.maximum(np.where(amax > 0, np.frexp(amax)[1] - 1 + 127, 0) - down, 1)
    scale = np.exp2(byte - 127.0)
    codes = (blocks / scale).astype(np.float32).astype(dtype).astype(np.float64)
    return np.moveaxis((codes * scale).reshape(v.shape), -1, axis)


WIDE = False


def mx_kscale(k):
    if not WIDE:
        return np.ones(k)
    levels = np.array([10, -10, 5, -5, 0])
    if k % 512:
        return np.exp2(np.random.permutation(np.resize(levels, k // 32))).repeat(32)
    a = np.empty((k // 512, 16))
    for p in range(k // 512):
        a[p, :8] = np.random.permutation(np.resize(levels, 8))
        for g in range(8):
            far = levels[np.abs(levels - a[p, g]) >= 10]
            a[p, g + 8] = far[np.random.randint(len(far))]
    return np.exp2(a.ravel()).repeat(32)


def f64(x):
    return np.asarray(x).astype(np.float64)


def striped(idx):
    return np.tile(idx.reshape(-1, 16).T, (8, 1)).astype(np.uint16)


def unstriped(offs):
    return offs[:16].T.reshape(-1).astype(np.int64)


def pack_weight(w):
    k, n = w.shape
    w = f64(np.asarray(w, np.float32).astype(ml_dtypes.bfloat16)).reshape(k // 32, 32, n)
    amax = np.abs(w).max(1)
    byte = np.clip(np.where(amax > 0, np.frexp(amax)[1] - 1 + 127 - 7, 1), 1, 254)
    scaled = (w * np.exp2(127.0 - byte)[:, None, :]).reshape(k, n).astype(np.float32)
    words = np.ascontiguousarray(scaled.reshape(k // 512, 128, 4, n).transpose(0, 1, 3, 2)).astype(ml_dtypes.float8_e4m3fn).view(np.uint8)
    return words, np.ascontiguousarray(byte.astype(np.uint8).reshape(k // 512, 16, n))


def unpack_weight(words, scales):
    g, p, n, _ = words.shape
    vals = np.ascontiguousarray(words).view(ml_dtypes.float8_e4m3fn).astype(np.float64) * np.repeat(np.exp2(scales.astype(np.float64) - 127.0), 8, axis=1)[..., None]
    return vals.transpose(0, 1, 3, 2).reshape(g * 512, n)


E2M1 = np.array([0.0, 0.5, 1.0, 1.5, 2.0, 3.0, 4.0, 6.0, -0.0, -0.5, -1.0, -1.5, -2.0, -3.0, -4.0, -6.0])


def pack_fp4(w):
    k, n = w.shape
    w = f64(np.asarray(w, np.float32).astype(ml_dtypes.bfloat16)).reshape(k // 32, 32, n)
    amax = np.abs(w).max(1)
    mant, ex = np.frexp(amax / 6.0)
    byte = np.clip(np.where(amax > 0, np.where(mant > 0.5, ex, ex - 1) + 127, 1), 1, 254)
    scaled = (w * np.exp2(127.0 - byte)[:, None, :]).reshape(k, n).astype(np.float32)
    c = np.ascontiguousarray(scaled.reshape(k // 512, 128, 4, n).transpose(0, 1, 3, 2)).astype(ml_dtypes.float4_e2m1fn).view(np.uint8) & 0xF
    words = (c[..., 0::2] | (c[..., 1::2] << 4)).reshape(k // 512, 128, 2 * n)
    return np.ascontiguousarray(words), np.ascontiguousarray(byte.astype(np.uint8).reshape(k // 512, 16, n))


def unpack_fp4(words, scales):
    g, _, n = scales.shape
    words = np.ascontiguousarray(words).reshape(g, 128, n, 2)
    nib = np.empty((g, 128, n, 4), np.uint8)
    nib[..., 0::2] = words & 0xF
    nib[..., 1::2] = words >> 4
    vals = E2M1[nib] * np.repeat(np.exp2(scales.astype(np.float64) - 127.0), 8, axis=1)[..., None]
    return vals.transpose(0, 1, 3, 2).reshape(g * 512, n)


def planes(y):
    n, m = y.shape
    v = y.astype(np.float32).astype(ml_dtypes.bfloat16).astype(np.float64).reshape(n // 32, 32, m)
    top = np.abs(v).max(1)
    byte = np.clip(np.where(top > 0, np.frexp(top)[1] - 1 + 127 - 7, 1), 1, 254)
    codes = (v * np.exp2(127.0 - byte)[:, None, :]).reshape(n, m).astype(np.float32).astype(ml_dtypes.float8_e4m3fn).view(np.uint8)
    words = codes.reshape(n // 512, 128, 4, m).transpose(0, 1, 3, 2)
    return np.ascontiguousarray(words), np.ascontiguousarray(byte.astype(np.uint8).reshape(n // 512, 16, m))


K, T, S, V, N, H = 512, 2048, 512, 512, 512, 512


def setup_inputs():
    n = np.random.standard_normal
    s = mx_kscale(K)[:, None]
    u = mx_kscale(S)
    packed_xT = pack_weight(n((K, T)) * s)
    packed_w1 = pack_fp4(n((K, H)) / np.sqrt(K) / s)
    packed_w2 = pack_fp4(n((K, H)) / np.sqrt(K) / s)
    return {
        "x_words": packed_xT[0],
        "x_scales": packed_xT[1],
        "w1_words": packed_w1[0],
        "w1_scales": packed_w1[1],
        "w2_words": packed_w2[0],
        "w2_scales": packed_w2[1],
        "gk": (np.random.uniform(0.5, 1.5, (H, 1)) * u[:, None]).astype(np.float32),
        "gq": (np.random.uniform(0.5, 1.5, (H, 1)) / u[:, None]).astype(np.float32),
        "wv": (n((K, N)) / np.sqrt(K) / s).astype(np.float32),
        "gi": (np.random.uniform(0.5, 1.5, (S, 1)) / u[:, None]).astype(np.float32),
        "res": (1.5 * n((N, V))).astype(np.float32),
        "gt": (np.random.uniform(0.5, 1.5, (S, 1)) * u[:, None]).astype(np.float32),
        "offs": striped(np.random.permutation(T)[:S]),
        "qs": striped(np.random.permutation(T)[:V]),
    }


def reference(x_words, x_scales, w1_words, w1_scales, w2_words, w2_scales, gk, gq, wv, gi, res, gt, offs, qs):
    xq = unpack_weight(x_words, x_scales)[:, unstriped(offs)]
    val = xq.T @ mxq(f64(wv), 0, "e4m3")
    zv = f64(gi) * val
    kf = unpack_fp4(w1_words, w1_scales).T @ xq
    z = f64(gk) * kf
    x_qs = unpack_weight(x_words, x_scales)[:, unstriped(qs)]
    qf = unpack_fp4(w2_words, w2_scales).T @ x_qs
    z2 = f64(gq) * qf
    s = 0.03125 * ((mxq(z, 0, "e4m3").T @ mxq(z2, 0, "e4m3")))
    e = np.exp(s - s.max(axis=1, keepdims=True))
    pq = e / e.sum(axis=1, keepdims=True)
    zp = f64(gt) * (16.0 * pq)
    out_0 = f64(res) + (mxq(zv, 0, "e4m3").T @ mxq(zp, 0, "e4m3"))
    return (out_0,) + planes(out_0)

@@ -1,0 +1,275 @@
+from contextlib import ExitStack
+
+import concourse.mybir as mybir
+from concourse.masks import make_identity
+
+K, T, S, V, N, H = 512, 2048, 512, 512, 512, 512
+FLOPS = 5 * 2 * 512 * 512 * 512
+
+F32 = mybir.dt.float32
+BF16 = mybir.dt.bfloat16
+I32 = mybir.dt.int32
+U32 = mybir.dt.uint32
+U16 = mybir.dt.uint16
+U8 = mybir.dt.uint8
+FP8X4 = mybir.dt.float8_e4m3fn_x4
+FP4X4 = mybir.dt.float4_e2m1fn_x4
+ACT = mybir.ActivationFunctionType
+ALU = mybir.AluOpType
+
+P = 128
+PACK = 4
+W = 512
+C = 128
+CHUNKS = W // C
+
+
+def tile_picked_listco_none_po_kernel(
+    tc, x_words, x_scales, w1_words, w1_scales, w2_words, w2_scales, gk, gq, wv, gi, res, gt, offs, qs,
+    out_0, out_1, out_2,
+):
+    nc = tc.nc
+
+    with ExitStack() as ctx:
+        lists = ctx.enter_context(tc.tile_pool(name="lists", bufs=1))
+        keep = ctx.enter_context(tc.tile_pool(name="keep", bufs=1))
+        psum = ctx.enter_context(tc.psum_pool(name="psum", bufs=1))
+
+        def sb(name, shape, dtype):
+            return keep.tile(shape, dtype, name=name, align_bytes=64)
+
+        def bank(tag, name):
+            return psum.tile([P, W], F32, name=name, tag=tag)
+
+        def load_plane(queue, plane, scales):
+            for q in range(4):
+                queue.dma_start(out=plane[32 * q : 32 * q + 4, :].bitcast(I32), in_=scales[0][4 * q : 4 * q + 4, :].bitcast(I32))
+
+        def mx(out, lhs, lhs_scale, rhs, rhs_scale):
+            nc.tensor.matmul_mx(out=out, lhsT=lhs, lhsT_scale=lhs_scale, rhs=rhs, rhs_scale=rhs_scale, start=True, stop=True)
+
+        def cols(c):
+            return slice(c * C, (c + 1) * C)
+
+        def woven(tile_ap):
+            return tile_ap.rearrange("p (c i t) -> p c t i", i=4, t=PACK)
+
+        def planes_walk(planes_ap):
+            return planes_ap.rearrange("p t (c i) -> p c t i", i=4)
+
+        qs_t = lists.tile([P, V // 16], U16, name="qs_t")
+        offs_t = lists.tile([P, S // 16], U16, name="offs_t")
+        xs = sb("xs", [P, T], U8)
+        xw = sb("xw", [P, T], U32)
+        nc.vector.memset(xs[:].bitcast(I32), 0)
+        nc.sync.dma_start(qs_t[:], qs)
+        nc.sync.dma_start(offs_t[:], offs)
+        load_plane(nc.scalar, xs, x_scales)
+        nc.sync.dma_start(out=xw[:].bitcast(I32), in_=x_words[0].rearrange("p n t -> p (n t)").bitcast(I32))
+
+        w2w = sb("w2w", [P, 2 * H], U8)
+        w1w = sb("w1w", [P, 2 * H], U8)
+        w2s = sb("w2s", [P, H], U8)
+        w1s = sb("w1s", [P, H], U8)
+        nc.vector.memset(w2s[:].bitcast(I32), 0)
+        nc.vector.memset(w1s[:].bitcast(I32), 0)
+        warm_in = sb("warm_in", [P, 8], F32)
+        warm_out = sb("warm_out", [P, 8], F32)
+        nc.vector.memset(warm_in[:], 0.0)
+        nc.sync.dma_start(out=w2w[:].bitcast(I32), in_=w2_words[0].bitcast(I32))
+        nc.scalar.activation(out=warm_out[:], in_=warm_in[:], func=ACT.Exp)
+        load_plane(nc.scalar, w2s, w2_scales)
+        nc.sync.dma_start(out=w1w[:].bitcast(I32), in_=w1_words[0].bitcast(I32))
+
+        rows = [sb("rows%d" % n, [P, P], F32) for n in range(2)]
+        ident = sb("ident", [P, P], F32)
+        for n, pair in enumerate(((gq, gk), (gi, gt))):
+            nc.gpsimd.memset(rows[n][:], 0.0)
+            for m, vec in enumerate(pair):
+                nc.gpsimd.dma_start(
+                    out=rows[n][4 * m : 4 * m + 4, :].rearrange("t (b r) -> t b r", r=8),
+                    in_=vec.rearrange("(b t r) o -> t b (r o)", t=PACK, r=8),
+                )
+            if n == 0:
+                make_identity(nc, ident[:])
+
+        wv_raw = [sb("wv_raw%d" % h, [P, PACK, W // 2], F32) for h in range(2)]
+        wv_rows = wv.rearrange("(p j) n -> p j n", j=PACK)
+        for h in range(2):
+            nc.sync.dma_start(out=wv_raw[h][:], in_=wv_rows[:, :, h * 256 : (h + 1) * 256])
+        load_plane(nc.sync, w1s, w1_scales)
+        res_t = sb("res_t", [P, PACK, V], F32)
+        nc.sync.dma_start(out=res_t[:], in_=res.rearrange("(p t) v -> p t v", t=PACK))
+
+        turned = bank("b2", "turned")
+        nc.tensor.transpose(turned[:, 0:P], rows[0][:], ident[:])
+        gains = sb("gains", [P, 8], F32)
+        nc.scalar.copy(out=gains[:], in_=turned[:, 0:8])
+        turned2 = bank("b3", "turned2")
+        nc.tensor.transpose(turned2[:, 0:P], rows[1][:], ident[:])
+        gi_t = sb("gi_t", [P, PACK], F32)
+        gt16 = sb("gt16", [P, PACK], F32)
+        nc.scalar.copy(out=gi_t[:], in_=turned2[:, 0:4])
+        nc.scalar.activation(out=gt16[:], in_=turned2[:, 4:8], func=ACT.Copy, scale=16.0)
+
+        qb = sb("qb", [P, V], U8)
+        qw = sb("qw", [P, V], U32)
+        ob_list = sb("ob_list", [P, S], U8)
+        ob = sb("ob", [P, S], U8)
+        ow = sb("ow", [P, S], U32)
+        w2wd = sb("w2wd", [P, 2 * H], U8)
+        w1wd = sb("w1wd", [P, 2 * H], U8)
+        w2sd = sb("w2sd", [P, H], U8)
+        w1sd = sb("w1sd", [P, H], U8)
+
+        def deal(engine, dealt, plain):
+            engine.tensor_copy(
+                out=dealt[:].bitcast(I32).rearrange("p (t b q) -> p t b q", t=PACK, b=16),
+                in_=plain[:].bitcast(I32).rearrange("p (b t q) -> p t b q", t=PACK, b=16),
+            )
+
+        nc.vector.tensor_copy(qb[:], xs[:].indirect(qs_t[:]))
+        nc.vector.tensor_copy(ob_list[:], xs[:].indirect(offs_t[:]))
+        deal(nc.vector, w2wd, w2w)
+        deal(nc.vector, w2sd, w2s)
+        nc.vector.tensor_copy(qw[:], xw[:].indirect(qs_t[:]))
+        nc.vector.tensor_copy(ow[:].rearrange("p (t b r) -> p b t r", t=PACK, b=16), xw[:].indirect(offs_t[:]))
+        deal(nc.vector, ob, ob_list)
+        deal(nc.vector, w1wd, w1w)
+        deal(nc.vector, w1sd, w1s)
+
+        wv_bf = sb("wv_bf", [P, PACK * N], BF16)
+        for h in range(2):
+            nc.scalar.copy(out=woven(wv_bf[:, h * 1024 : (h + 1) * 1024]), in_=planes_walk(wv_raw[h][:]))
+
+        z2_bf = sb("z2_bf", [P, PACK * V], BF16)
+        z_planes = sb("z_planes", [P, PACK, S], BF16)
+        gq_spread = gains[:, 0:4].rearrange("p (o t) -> p o t", o=1).to_broadcast([P, C, PACK])
+
+        def query_chunk(c):
+            acc = bank("a%d" % c, "qf%d" % c)
+            for t in range(PACK):
+                mx(acc[:, cols(t)], w2wd[:, 2 * C * t : 2 * C * (t + 1)].bitcast(FP4X4), w2sd[:, cols(t)],
+                   qw[:, cols(c)].bitcast(FP8X4), qb[:, cols(c)])
+            nc.vector.tensor_tensor(
+                out=z2_bf[:, c * W : (c + 1) * W].rearrange("p (n t) -> p n t", t=PACK),
+                in0=acc[:].rearrange("p (t n) -> p n t", t=PACK), in1=gq_spread, op=ALU.mult)
+
+        def key_tile(t):
+            acc = bank("b%d" % t, "kf%d" % t)
+            mx(acc[:], w1wd[:, 2 * C * t : 2 * C * (t + 1)].bitcast(FP4X4), w1sd[:, cols(t)], ow[:].bitcast(FP8X4), ob[:])
+            nc.scalar.activation(out=z_planes[:, t, :], in_=acc[:], func=ACT.Copy, scale=gains[:, 4 + t : 5 + t])
+
+        wv_q = sb("wv_q", [P, N], U32)
+        wv_s = sb("wv_s", [P, N], U8)
+        query_chunk(0)
+        query_chunk(1)
+        key_tile(0)
+        nc.vector.quantize_mx(out=wv_q[:].bitcast(FP8X4), scales=wv_s[:], in_=wv_bf[:])
+        query_chunk(2)
+        key_tile(1)
+        query_chunk(3)
+        key_tile(2)
+        key_tile(3)
+        z2_q = sb("z2_q", [P, V], U32)
+        z2_s = sb("z2_s", [P, V], U8)
+        nc.vector.quantize_mx(out=z2_q[:].bitcast(FP8X4), scales=z2_s[:], in_=z2_bf[:])
+
+        zv_planes = sb("zv_planes", [P, PACK, N], BF16)
+        for t in range(PACK):
+            acc = bank("a%d" % t, "val%d" % t)
+            mx(acc[:], ow[:, cols(t)].bitcast(FP8X4), ob[:, cols(t)], wv_q[:].bitcast(FP8X4), wv_s[:])
+            nc.scalar.activation(
+                out=zv_planes[:, t, :].rearrange("p (u m) -> p u m", u=PACK),
+                in_=acc[:].rearrange("p (m u) -> p u m", u=PACK),
+                func=ACT.Copy, scale=gi_t[:, t : t + 1])
+
+        z_bf = [sb("z_bf%d" % c, [P, W], BF16) for c in range(CHUNKS)]
+        z_q = [sb("z_q%d" % c, [P, C], U32) for c in range(CHUNKS)]
+        z_s = [sb("z_s%d" % c, [P, C], U8) for c in range(CHUNKS)]
+        neg = [sb("neg%d" % c, [P, V], F32) for c in range(CHUNKS)]
+        low = [sb("low%d" % c, [P, 1], F32) for c in range(CHUNKS)]
+        total = sb("total", [P, PACK], F32)
+        e = sb("e", [P, PACK, V], F32)
+
+        def weave_keys(c):
+            nc.vector.tensor_copy(out=woven(z_bf[c][:]), in_=planes_walk(z_planes[:, :, cols(c)]))
+
+        scores = []
+
+        def score(c):
+            nc.vector.quantize_mx(out=z_q[c][:].bitcast(FP8X4), scales=z_s[c][:], in_=z_bf[c][:])
+            acc = bank("b%d" % c, "s%d" % c)
+            mx(acc[:], z_q[c][:].bitcast(FP8X4), z_s[c][:], z2_q[:].bitcast(FP8X4), z2_s[:])
+            scores.append(acc)
+
+        def soft(c):
+            nc.vector.tensor_scalar(out=neg[c][:], in0=scores[c][:], scalar1=-0.03125, scalar2=None,
+                                    op0=ALU.mult, op1=ALU.min, accum_out=low[c][:])
+            nc.scalar.activation(out=e[:, c, :], in_=neg[c][:], func=ACT.Exp, bias=low[c][:], scale=-1.0,
+                                 accum_out=total[:, c : c + 1])
+
+        weave_keys(0)
+        for c in range(CHUNKS):
+            if c + 1 < CHUNKS:
+                weave_keys(c + 1)
+            score(c)
+        for c in range(CHUNKS):
+            soft(c)
+
+        zv_bf = sb("zv_bf", [P, PACK * N], BF16)
+        zv_q = sb("zv_q", [P, N], U32)
+        zv_s = sb("zv_s", [P, N], U8)
+        nc.vector.tensor_copy(out=woven(zv_bf[:]), in_=planes_walk(zv_planes[:]))
+        inv = sb("inv", [P, PACK], F32)
+        factor = sb("factor", [P, PACK], F32)
+        nc.vector.reciprocal(out=inv[:], in_=total[:])
+        nc.vector.quantize_mx(out=zv_q[:].bitcast(FP8X4), scales=zv_s[:], in_=zv_bf[:])
+        nc.vector.tensor_tensor(out=factor[:], in0=inv[:], in1=gt16[:], op=ALU.mult)
+        factor_spread = factor[:].rearrange("p (a t b) -> p a t b", a=1, b=1).to_broadcast([P, C // 4, PACK, 4])
+
+        zp_bf = [sb("zp_bf%d" % c, [P, W], BF16) for c in range(CHUNKS)]
+        zp_q = [sb("zp_q%d" % c, [P, C], U32) for c in range(CHUNKS)]
+        zp_s = [sb("zp_s%d" % c, [P, C], U8) for c in range(CHUNKS)]
+        y = [sb("y%d" % c, [P, PACK, C], F32) for c in range(CHUNKS)]
+        y_bf = [sb("y_bf%d" % c, [P, W], BF16) for c in range(CHUNKS)]
+        y_q = sb("y_q", [P, V], U32)
+        y_s = sb("y_s", [P, V], U8)
+        out_rows = out_0.rearrange("(p t) v -> p t v", t=PACK)
+        out_words = out_1[0].rearrange("p n t -> p (n t)").bitcast(I32)
+        sums = []
+
+        def weigh(c):
+            nc.vector.tensor_tensor(out=woven(zp_bf[c][:]), in0=planes_walk(e[:, :, cols(c)]), in1=factor_spread, op=ALU.mult)
+
+        def product(c):
+            nc.vector.quantize_mx(out=zp_q[c][:].bitcast(FP8X4), scales=zp_s[c][:], in_=zp_bf[c][:])
+            acc = bank("a%d" % c, "y_acc%d" % c)
+            for u in range(PACK):
+                mx(acc[:, cols(u)], zv_q[:, cols(u)].bitcast(FP8X4), zv_s[:, cols(u)], zp_q[c][:].bitcast(FP8X4), zp_s[c][:])
+            sums.append(acc)
+
+        def finish(c):
+            nc.vector.tensor_tensor(out=y[c][:], in0=sums[c][:].rearrange("p (u n) -> p u n", u=PACK),
+                                    in1=res_t[:, :, cols(c)], op=ALU.add)
+            nc.sync.dma_start(out=out_rows[:, :, cols(c)], in_=y[c][:])
+            nc.scalar.copy(out=woven(y_bf[c][:]), in_=planes_walk(y[c][:]))
+
+        def hand_on(c):
+            nc.vector.quantize_mx(out=y_q[:, cols(c)].bitcast(FP8X4), scales=y_s[:, cols(c)], in_=y_bf[c][:])
+            if c % 2 == 1:
+                half = slice((c - 1) * C, (c + 1) * C)
+                nc.sync.dma_start(out=out_words[:, half], in_=y_q[:, half].bitcast(I32))
+
+        for step in range(CHUNKS + 3):
+            if step < CHUNKS:
+                weigh(step)
+            if 0 <= step - 1 < CHUNKS:
+                product(step - 1)
+            if 0 <= step - 2 < CHUNKS:
+                finish(step - 2)
+            if 0 <= step - 3 < CHUNKS:
+                hand_on(step - 3)
+        for q in range(4):
+            queue = nc.scalar if q % 2 else nc.sync
+            queue.dma_start(out=out_2[0][4 * q : 4 * q + 4, :].bitcast(I32), in_=y_s[32 * q : 32 * q + 4, :].bitcast(I32))

@@ -41,9 +41,9 @@ def tile_picked_listco_none_po_kernel(
         def bank(tag, name):
             return psum.tile([P, W], F32, name=name, tag=tag)
 
-        def load_plane(queue, plane, scales):
+        def load_plane(plane, scales):
             for q in range(4):
-                queue.dma_start(out=plane[32 * q : 32 * q + 4, :].bitcast(I32), in_=scales[0][4 * q : 4 * q + 4, :].bitcast(I32))
+                nc.sync.dma_start(out=plane[32 * q : 32 * q + 4, :].bitcast(I32), in_=scales[0][4 * q : 4 * q + 4, :].bitcast(I32))
 
         def mx(out, lhs, lhs_scale, rhs, rhs_scale):
             nc.tensor.matmul_mx(out=out, lhsT=lhs, lhsT_scale=lhs_scale, rhs=rhs, rhs_scale=rhs_scale, start=True, stop=True)
@@ -61,56 +61,52 @@ def tile_picked_listco_none_po_kernel(
         offs_t = lists.tile([P, S // 16], U16, name="offs_t")
         xs = sb("xs", [P, T], U8)
         xw = sb("xw", [P, T], U32)
-        nc.vector.memset(xs[:].bitcast(I32), 0)
-        nc.sync.dma_start(qs_t[:], qs)
-        nc.sync.dma_start(offs_t[:], offs)
-        load_plane(nc.scalar, xs, x_scales)
-        nc.sync.dma_start(out=xw[:].bitcast(I32), in_=x_words[0].rearrange("p n t -> p (n t)").bitcast(I32))
-
         w2w = sb("w2w", [P, 2 * H], U8)
         w1w = sb("w1w", [P, 2 * H], U8)
         w2s = sb("w2s", [P, H], U8)
         w1s = sb("w1s", [P, H], U8)
-        nc.vector.memset(w2s[:].bitcast(I32), 0)
-        nc.vector.memset(w1s[:].bitcast(I32), 0)
         warm_in = sb("warm_in", [P, 8], F32)
         warm_out = sb("warm_out", [P, 8], F32)
-        nc.vector.memset(warm_in[:], 0.0)
-        nc.sync.dma_start(out=w2w[:].bitcast(I32), in_=w2_words[0].bitcast(I32))
-        nc.scalar.activation(out=warm_out[:], in_=warm_in[:], func=ACT.Exp)
-        load_plane(nc.scalar, w2s, w2_scales)
-        nc.sync.dma_start(out=w1w[:].bitcast(I32), in_=w1_words[0].bitcast(I32))
-
         rows = [sb("rows%d" % n, [P, P], F32) for n in range(2)]
         ident = sb("ident", [P, P], F32)
-        for n, pair in enumerate(((gq, gk), (gi, gt))):
-            nc.gpsimd.memset(rows[n][:], 0.0)
-            for m, vec in enumerate(pair):
-                nc.gpsimd.dma_start(
-                    out=rows[n][4 * m : 4 * m + 4, :].rearrange("t (b r) -> t b r", r=8),
-                    in_=vec.rearrange("(b t r) o -> t b (r o)", t=PACK, r=8),
-                )
-            if n == 0:
-                make_identity(nc, ident[:])
+        nc.gpsimd.memset(xs[:].bitcast(I32), 0)
+        nc.vector.memset(rows[0][:], 0.0)
+        nc.vector.memset(warm_in[:], 0.0)
+        nc.vector.memset(w2s[:].bitcast(I32), 0)
+        nc.vector.memset(w1s[:].bitcast(I32), 0)
+        nc.vector.memset(rows[1][:], 0.0)
+        make_identity(nc, ident[:])
+        nc.scalar.activation(out=warm_out[:], in_=warm_in[:], func=ACT.Exp)
 
-        wv_raw = [sb("wv_raw%d" % h, [P, PACK, W // 2], F32) for h in range(2)]
+        def load_rows(queue, n, m, vec):
+            queue.dma_start(
+                out=rows[n][4 * m : 4 * m + 4, :].rearrange("t (b r) -> t b r", r=8),
+                in_=vec.rearrange("(b t r) o -> t b (r o)", t=PACK, r=8),
+            )
+
+        wv_raw = [sb("wv_raw%d" % h, [P, PACK, N // 2], F32) for h in range(2)]
         wv_rows = wv.rearrange("(p j) n -> p j n", j=PACK)
-        for h in range(2):
-            nc.sync.dma_start(out=wv_raw[h][:], in_=wv_rows[:, :, h * 256 : (h + 1) * 256])
-        load_plane(nc.sync, w1s, w1_scales)
         res_t = sb("res_t", [P, PACK, V], F32)
+        nc.sync.dma_start(qs_t[:], qs)
+        load_plane(xs, x_scales)
+        nc.sync.dma_start(offs_t[:], offs)
+        load_rows(nc.sync, 0, 0, gq)
+        nc.sync.dma_start(out=xw[:].bitcast(I32), in_=x_words[0].rearrange("p n t -> p (n t)").bitcast(I32))
+        load_rows(nc.sync, 0, 1, gk)
+        nc.sync.dma_start(out=w2w[:].bitcast(I32), in_=w2_words[0].bitcast(I32))
+        load_plane(w2s, w2_scales)
+        nc.sync.dma_start(out=wv_raw[0][:], in_=wv_rows[:, :, 0:256])
+        nc.sync.dma_start(out=w1w[:].bitcast(I32), in_=w1_words[0].bitcast(I32))
+        load_plane(w1s, w1_scales)
+        nc.sync.dma_start(out=wv_raw[1][:], in_=wv_rows[:, :, 256:512])
+        load_rows(nc.sync, 1, 0, gi)
+        load_rows(nc.sync, 1, 1, gt)
         nc.sync.dma_start(out=res_t[:], in_=res.rearrange("(p t) v -> p t v", t=PACK))
 
-        turned = bank("b2", "turned")
+        turned = bank("b0", "turned")
         nc.tensor.transpose(turned[:, 0:P], rows[0][:], ident[:])
         gains = sb("gains", [P, 8], F32)
         nc.scalar.copy(out=gains[:], in_=turned[:, 0:8])
-        turned2 = bank("b3", "turned2")
-        nc.tensor.transpose(turned2[:, 0:P], rows[1][:], ident[:])
-        gi_t = sb("gi_t", [P, PACK], F32)
-        gt16 = sb("gt16", [P, PACK], F32)
-        nc.scalar.copy(out=gi_t[:], in_=turned2[:, 0:4])
-        nc.scalar.activation(out=gt16[:], in_=turned2[:, 4:8], func=ACT.Copy, scale=16.0)
 
         qb = sb("qb", [P, V], U8)
         qw = sb("qw", [P, V], U32)
@@ -130,61 +126,67 @@ def tile_picked_listco_none_po_kernel(
 
         nc.vector.tensor_copy(qb[:], xs[:].indirect(qs_t[:]))
         nc.vector.tensor_copy(ob_list[:], xs[:].indirect(offs_t[:]))
-        deal(nc.vector, w2wd, w2w)
-        deal(nc.vector, w2sd, w2s)
         nc.vector.tensor_copy(qw[:], xw[:].indirect(qs_t[:]))
-        nc.vector.tensor_copy(ow[:].rearrange("p (t b r) -> p b t r", t=PACK, b=16), xw[:].indirect(offs_t[:]))
+        deal(nc.gpsimd, w2wd, w2w)
+        deal(nc.gpsimd, w2sd, w2s)
         deal(nc.vector, ob, ob_list)
-        deal(nc.vector, w1wd, w1w)
-        deal(nc.vector, w1sd, w1s)
+        nc.vector.tensor_copy(ow[:].rearrange("p (t b r) -> p b t r", t=PACK, b=16), xw[:].indirect(offs_t[:]))
+        deal(nc.gpsimd, w1wd, w1w)
+        deal(nc.gpsimd, w1sd, w1s)
 
         wv_bf = sb("wv_bf", [P, PACK * N], BF16)
-        for h in range(2):
-            nc.scalar.copy(out=woven(wv_bf[:, h * 1024 : (h + 1) * 1024]), in_=planes_walk(wv_raw[h][:]))
+        nc.scalar.copy(out=woven(wv_bf[:, 0:1024]), in_=planes_walk(wv_raw[0][:]))
+        nc.gpsimd.tensor_scalar(out=wv_bf[:, 1024:2048].rearrange("p (n t) -> p n t", t=PACK),
+                                in0=wv_raw[1][:].rearrange("p t n -> p n t"), scalar1=1.0, scalar2=0.0,
+                                op0=ALU.mult, op1=ALU.add)
 
         z2_bf = sb("z2_bf", [P, PACK * V], BF16)
-        z_planes = sb("z_planes", [P, PACK, S], BF16)
+        z_planes = sb("z_planes", [P, PACK, S // 2], BF16)
         gq_spread = gains[:, 0:4].rearrange("p (o t) -> p o t", o=1).to_broadcast([P, C, PACK])
 
-        def query_chunk(c):
-            acc = bank("a%d" % c, "qf%d" % c)
-            for t in range(PACK):
-                mx(acc[:, cols(t)], w2wd[:, 2 * C * t : 2 * C * (t + 1)].bitcast(FP4X4), w2sd[:, cols(t)],
-                   qw[:, cols(c)].bitcast(FP8X4), qb[:, cols(c)])
-            nc.vector.tensor_tensor(
-                out=z2_bf[:, c * W : (c + 1) * W].rearrange("p (n t) -> p n t", t=PACK),
-                in0=acc[:].rearrange("p (t n) -> p n t", t=PACK), in1=gq_spread, op=ALU.mult)
+        gk_spread = gains[:, 4:8].rearrange("p (o t) -> p o t", o=1).to_broadcast([P, C, PACK])
+        z_bf = [sb("z_bf%d" % c, [P, W], BF16) for c in range(CHUNKS)]
 
-        def key_tile(t):
-            acc = bank("b%d" % t, "kf%d" % t)
-            mx(acc[:], w1wd[:, 2 * C * t : 2 * C * (t + 1)].bitcast(FP4X4), w1sd[:, cols(t)], ow[:].bitcast(FP8X4), ob[:])
-            nc.scalar.activation(out=z_planes[:, t, :], in_=acc[:], func=ACT.Copy, scale=gains[:, 4 + t : 5 + t])
+        def chunk_product(tag, name, words, plane, x_words_t, x_plane, c):
+            acc = bank(tag, name)
+            for t in range(PACK):
+                mx(acc[:, cols(t)], words[:, 2 * C * t : 2 * C * (t + 1)].bitcast(FP4X4), plane[:, cols(t)],
+                   x_words_t[:, cols(c)].bitcast(FP8X4), x_plane[:, cols(c)])
+            return acc
+
+        def weigh_woven(dst, acc, spread):
+            nc.vector.tensor_tensor(out=dst.rearrange("p (n t) -> p n t", t=PACK),
+                                    in0=acc[:].rearrange("p (t n) -> p n t", t=PACK), in1=spread, op=ALU.mult)
 
         wv_q = sb("wv_q", [P, N], U32)
         wv_s = sb("wv_s", [P, N], U8)
-        query_chunk(0)
-        query_chunk(1)
-        key_tile(0)
-        nc.vector.quantize_mx(out=wv_q[:].bitcast(FP8X4), scales=wv_s[:], in_=wv_bf[:])
-        query_chunk(2)
-        key_tile(1)
-        query_chunk(3)
-        key_tile(2)
-        key_tile(3)
+        for c in range(CHUNKS):
+            acc = chunk_product("a%d" % c, "qf%d" % c, w2wd, w2sd, qw, qb, c)
+            weigh_woven(z2_bf[:, c * W : (c + 1) * W], acc, gq_spread)
+        for pair in range(2):
+            acc = bank("b%d" % pair, "kf_hi%d" % pair)
+            for u in range(2):
+                t = 2 * pair + u
+                mx(acc[:, 256 * u : 256 * (u + 1)], w1wd[:, 2 * C * t : 2 * C * (t + 1)].bitcast(FP4X4), w1sd[:, cols(t)],
+                   ow[:, 256:512].bitcast(FP8X4), ob[:, 256:512])
+            for u in range(2):
+                t = 2 * pair + u
+                nc.scalar.activation(out=z_planes[:, t, :], in_=acc[:, 256 * u : 256 * (u + 1)], func=ACT.Copy,
+                                     scale=gains[:, 4 + t : 5 + t])
+        kf_lo = [chunk_product("b%d" % (2 + c), "kf_lo%d" % c, w1wd, w1sd, ow, ob, c) for c in range(2)]
         z2_q = sb("z2_q", [P, V], U32)
         z2_s = sb("z2_s", [P, V], U8)
         nc.vector.quantize_mx(out=z2_q[:].bitcast(FP8X4), scales=z2_s[:], in_=z2_bf[:])
+        for h in range(2):
+            nc.vector.quantize_mx(out=wv_q[:, 256 * h : 256 * (h + 1)].bitcast(FP8X4), scales=wv_s[:, 256 * h : 256 * (h + 1)],
+                                  in_=wv_bf[:, 1024 * h : 1024 * (h + 1)])
+        turned2 = bank("a0", "turned2")
+        nc.tensor.transpose(turned2[:, 0:P], rows[1][:], ident[:])
+        gi_t = sb("gi_t", [P, PACK], F32)
+        gt16 = sb("gt16", [P, PACK], F32)
+        nc.scalar.copy(out=gi_t[:], in_=turned2[:, 0:4])
+        nc.scalar.activation(out=gt16[:], in_=turned2[:, 4:8], func=ACT.Copy, scale=16.0)
 
-        zv_planes = sb("zv_planes", [P, PACK, N], BF16)
-        for t in range(PACK):
-            acc = bank("a%d" % t, "val%d" % t)
-            mx(acc[:], ow[:, cols(t)].bitcast(FP8X4), ob[:, cols(t)], wv_q[:].bitcast(FP8X4), wv_s[:])
-            nc.scalar.activation(
-                out=zv_planes[:, t, :].rearrange("p (u m) -> p u m", u=PACK),
-                in_=acc[:].rearrange("p (m u) -> p u m", u=PACK),
-                func=ACT.Copy, scale=gi_t[:, t : t + 1])
-
-        z_bf = [sb("z_bf%d" % c, [P, W], BF16) for c in range(CHUNKS)]
         z_q = [sb("z_q%d" % c, [P, C], U32) for c in range(CHUNKS)]
         z_s = [sb("z_s%d" % c, [P, C], U8) for c in range(CHUNKS)]
         neg = [sb("neg%d" % c, [P, V], F32) for c in range(CHUNKS)]
@@ -193,13 +195,16 @@ def tile_picked_listco_none_po_kernel(
         e = sb("e", [P, PACK, V], F32)
 
         def weave_keys(c):
-            nc.vector.tensor_copy(out=woven(z_bf[c][:]), in_=planes_walk(z_planes[:, :, cols(c)]))
+            if c < 2:
+                weigh_woven(z_bf[c][:], kf_lo[c], gk_spread)
+            else:
+                nc.vector.tensor_copy(out=woven(z_bf[c][:]), in_=planes_walk(z_planes[:, :, cols(c - 2)]))
 
         scores = []
 
         def score(c):
             nc.vector.quantize_mx(out=z_q[c][:].bitcast(FP8X4), scales=z_s[c][:], in_=z_bf[c][:])
-            acc = bank("b%d" % c, "s%d" % c)
+            acc = bank("a%d" % c, "s%d" % c)
             mx(acc[:], z_q[c][:].bitcast(FP8X4), z_s[c][:], z2_q[:].bitcast(FP8X4), z2_s[:])
             scores.append(acc)
 
@@ -210,17 +215,36 @@ def tile_picked_listco_none_po_kernel(
                                  accum_out=total[:, c : c + 1])
 
         weave_keys(0)
+        weave_keys(1)
+        zv_planes = [sb("zv_planes%d" % h, [P, PACK, N // 2], BF16) for h in range(2)]
+        zv_bf = sb("zv_bf", [P, PACK * N], BF16)
+        for h in range(2):
+            for pair in range(2):
+                acc = bank("b%d" % (2 * h + pair), "val%d_%d" % (h, pair))
+                for k in range(2):
+                    t = 2 * pair + k
+                    mx(acc[:, 256 * k : 256 * (k + 1)], ow[:, cols(t)].bitcast(FP8X4), ob[:, cols(t)],
+                       wv_q[:, 256 * h : 256 * (h + 1)].bitcast(FP8X4), wv_s[:, 256 * h : 256 * (h + 1)])
+                for k in range(2):
+                    t = 2 * pair + k
+                    nc.scalar.activation(
+                        out=zv_planes[h][:, t, :].rearrange("p (u m) -> p u m", u=PACK),
+                        in_=acc[:, 256 * k : 256 * (k + 1)].rearrange("p (m u) -> p u m", u=PACK),
+                        func=ACT.Copy, scale=gi_t[:, t : t + 1])
+            nc.gpsimd.tensor_scalar(
+                out=zv_bf[:].rearrange("p (u h m t) -> p h u m t", u=PACK, h=2, t=PACK)[:, h],
+                in0=zv_planes[h][:].rearrange("p t (u m) -> p u m t", u=PACK), scalar1=1.0, scalar2=0.0,
+                op0=ALU.mult, op1=ALU.add)
+
         for c in range(CHUNKS):
-            if c + 1 < CHUNKS:
-                weave_keys(c + 1)
             score(c)
+            if c + 2 < CHUNKS:
+                weave_keys(c + 2)
         for c in range(CHUNKS):
             soft(c)
 
-        zv_bf = sb("zv_bf", [P, PACK * N], BF16)
         zv_q = sb("zv_q", [P, N], U32)
         zv_s = sb("zv_s", [P, N], U8)
-        nc.vector.tensor_copy(out=woven(zv_bf[:]), in_=planes_walk(zv_planes[:]))
         inv = sb("inv", [P, PACK], F32)
         factor = sb("factor", [P, PACK], F32)
         nc.vector.reciprocal(out=inv[:], in_=total[:])
@@ -239,12 +263,19 @@ def tile_picked_listco_none_po_kernel(
         out_words = out_1[0].rearrange("p n t -> p (n t)").bitcast(I32)
         sums = []
 
+        zp_planes = sb("zp_planes", [P, PACK, V // 2], BF16)
+        for t in range(PACK):
+            nc.scalar.activation(out=zp_planes[:, t, :], in_=e[:, t, 256:512], func=ACT.Copy, scale=factor[:, t : t + 1])
+
         def weigh(c):
-            nc.vector.tensor_tensor(out=woven(zp_bf[c][:]), in0=planes_walk(e[:, :, cols(c)]), in1=factor_spread, op=ALU.mult)
+            if c < 2:
+                nc.vector.tensor_tensor(out=woven(zp_bf[c][:]), in0=planes_walk(e[:, :, cols(c)]), in1=factor_spread, op=ALU.mult)
+            else:
+                nc.vector.tensor_copy(out=woven(zp_bf[c][:]), in_=planes_walk(zp_planes[:, :, cols(c - 2)]))
 
         def product(c):
             nc.vector.quantize_mx(out=zp_q[c][:].bitcast(FP8X4), scales=zp_s[c][:], in_=zp_bf[c][:])
-            acc = bank("a%d" % c, "y_acc%d" % c)
+            acc = bank("b%d" % c, "y_acc%d" % c)
             for u in range(PACK):
                 mx(acc[:, cols(u)], zv_q[:, cols(u)].bitcast(FP8X4), zv_s[:, cols(u)], zp_q[c][:].bitcast(FP8X4), zp_s[c][:])
             sums.append(acc)
@@ -257,9 +288,7 @@ def tile_picked_listco_none_po_kernel(
 
         def hand_on(c):
             nc.vector.quantize_mx(out=y_q[:, cols(c)].bitcast(FP8X4), scales=y_s[:, cols(c)], in_=y_bf[c][:])
-            if c % 2 == 1:
-                half = slice((c - 1) * C, (c + 1) * C)
-                nc.sync.dma_start(out=out_words[:, half], in_=y_q[:, half].bitcast(I32))
+            nc.sync.dma_start(out=out_words[:, cols(c)], in_=y_q[:, cols(c)].bitcast(I32))
 
         for step in range(CHUNKS + 3):
             if step < CHUNKS:

@@ -21,6 +21,7 @@ P = 128
 PACK = 4
 W = 512
 C = 128
+HALF = 256
 CHUNKS = W // C
 
 
@@ -33,17 +34,21 @@ def tile_picked_listco_none_po_kernel(
     with ExitStack() as ctx:
         lists = ctx.enter_context(tc.tile_pool(name="lists", bufs=1))
         keep = ctx.enter_context(tc.tile_pool(name="keep", bufs=1))
+        placed = ctx.enter_context(tc.tile_pool(name="placed", bufs=1))
         psum = ctx.enter_context(tc.psum_pool(name="psum", bufs=1))
 
-        def sb(name, shape, dtype):
-            return keep.tile(shape, dtype, name=name, align_bytes=64)
+        def sb(name, shape, dtype, tag=None):
+            return keep.tile(shape, dtype, name=name, tag=tag or name, align_bytes=64)
+
+        def at(offset, name, shape, dtype):
+            return placed.tile(shape, dtype, name=name, align_bytes=64, offset=offset)
 
         def bank(tag, name):
             return psum.tile([P, W], F32, name=name, tag=tag)
 
-        def load_plane(plane, scales):
+        def load_plane(plane, scales, queues):
             for q in range(4):
-                nc.sync.dma_start(out=plane[32 * q : 32 * q + 4, :].bitcast(I32), in_=scales[0][4 * q : 4 * q + 4, :].bitcast(I32))
+                queues[q].dma_start(out=plane[32 * q : 32 * q + 4, :].bitcast(I32), in_=scales[0][4 * q : 4 * q + 4, :].bitcast(I32))
 
         def mx(out, lhs, lhs_scale, rhs, rhs_scale):
             nc.tensor.matmul_mx(out=out, lhsT=lhs, lhsT_scale=lhs_scale, rhs=rhs, rhs_scale=rhs_scale, start=True, stop=True)
@@ -51,59 +56,62 @@ def tile_picked_listco_none_po_kernel(
         def cols(c):
             return slice(c * C, (c + 1) * C)
 
+        def half(h):
+            return slice(h * HALF, (h + 1) * HALF)
+
         def woven(tile_ap):
             return tile_ap.rearrange("p (c i t) -> p c t i", i=4, t=PACK)
 
         def planes_walk(planes_ap):
             return planes_ap.rearrange("p t (c i) -> p c t i", i=4)
 
+        def pool_weave(dst, src):
+            nc.gpsimd.tensor_scalar(out=dst, in0=src, scalar1=1.0, scalar2=0.0, op0=ALU.mult, op1=ALU.add)
+
         qs_t = lists.tile([P, V // 16], U16, name="qs_t")
         offs_t = lists.tile([P, S // 16], U16, name="offs_t")
         xs = sb("xs", [P, T], U8)
         xw = sb("xw", [P, T], U32)
-        w2w = sb("w2w", [P, 2 * H], U8)
+        w2w = at(0, "w2w", [P, 2 * H], U8)
+        w2s = at(1024, "w2s", [P, H], U8)
         w1w = sb("w1w", [P, 2 * H], U8)
-        w2s = sb("w2s", [P, H], U8)
-        w1s = sb("w1s", [P, H], U8)
-        warm_in = sb("warm_in", [P, 8], F32)
-        warm_out = sb("warm_out", [P, 8], F32)
+        w1s = at(2048, "w1s", [P, H], U8)
         rows = [sb("rows%d" % n, [P, P], F32) for n in range(2)]
         ident = sb("ident", [P, P], F32)
         nc.gpsimd.memset(xs[:].bitcast(I32), 0)
         nc.vector.memset(rows[0][:], 0.0)
-        nc.vector.memset(warm_in[:], 0.0)
         nc.vector.memset(w2s[:].bitcast(I32), 0)
         nc.vector.memset(w1s[:].bitcast(I32), 0)
-        nc.vector.memset(rows[1][:], 0.0)
         make_identity(nc, ident[:])
-        nc.scalar.activation(out=warm_out[:], in_=warm_in[:], func=ACT.Exp)
 
-        def load_rows(queue, n, m, vec):
+        def load_rows(n, m, vec, queue=nc.sync):
             queue.dma_start(
                 out=rows[n][4 * m : 4 * m + 4, :].rearrange("t (b r) -> t b r", r=8),
                 in_=vec.rearrange("(b t r) o -> t b (r o)", t=PACK, r=8),
             )
 
-        wv_raw = [sb("wv_raw%d" % h, [P, PACK, N // 2], F32) for h in range(2)]
+        wv_raw = [sb("wv_raw%d" % h, [P, PACK, HALF], F32) for h in range(2)]
         wv_rows = wv.rearrange("(p j) n -> p j n", j=PACK)
         res_t = sb("res_t", [P, PACK, V], F32)
+        on_sync = [nc.sync] * 4
         nc.sync.dma_start(qs_t[:], qs)
-        load_plane(xs, x_scales)
+        load_plane(xs, x_scales, on_sync)
         nc.sync.dma_start(offs_t[:], offs)
-        load_rows(nc.sync, 0, 0, gq)
+        load_rows(0, 0, gq)
+        nc.scalar.activation(out=rows[1][:], in_=ident[:], func=ACT.Exp)
         nc.sync.dma_start(out=xw[:].bitcast(I32), in_=x_words[0].rearrange("p n t -> p (n t)").bitcast(I32))
-        load_rows(nc.sync, 0, 1, gk)
         nc.sync.dma_start(out=w2w[:].bitcast(I32), in_=w2_words[0].bitcast(I32))
-        load_plane(w2s, w2_scales)
-        nc.sync.dma_start(out=wv_raw[0][:], in_=wv_rows[:, :, 0:256])
+        load_rows(0, 1, gk)
+        load_plane(w2s, w2_scales, on_sync)
+        nc.sync.dma_start(out=wv_raw[0][:], in_=wv_rows[:, :, half(0)])
+        nc.sync.dma_start(out=wv_raw[1][:], in_=wv_rows[:, :, half(1)])
         nc.sync.dma_start(out=w1w[:].bitcast(I32), in_=w1_words[0].bitcast(I32))
-        load_plane(w1s, w1_scales)
-        nc.sync.dma_start(out=wv_raw[1][:], in_=wv_rows[:, :, 256:512])
-        load_rows(nc.sync, 1, 0, gi)
-        load_rows(nc.sync, 1, 1, gt)
+        load_plane(w1s, w1_scales, on_sync)
+        load_rows(1, 0, gi)
+        load_rows(1, 1, gt)
         nc.sync.dma_start(out=res_t[:], in_=res.rearrange("(p t) v -> p t v", t=PACK))
 
-        turned = bank("b0", "turned")
+        turned = bank("b3", "turned")
         nc.tensor.transpose(turned[:, 0:P], rows[0][:], ident[:])
         gains = sb("gains", [P, 8], F32)
         nc.scalar.copy(out=gains[:], in_=turned[:, 0:8])
@@ -112,7 +120,6 @@ def tile_picked_listco_none_po_kernel(
         qw = sb("qw", [P, V], U32)
         ob_list = sb("ob_list", [P, S], U8)
         ob = sb("ob", [P, S], U8)
-        ow = sb("ow", [P, S], U32)
         w2wd = sb("w2wd", [P, 2 * H], U8)
         w1wd = sb("w1wd", [P, 2 * H], U8)
         w2sd = sb("w2sd", [P, H], U8)
@@ -126,26 +133,22 @@ def tile_picked_listco_none_po_kernel(
 
         nc.vector.tensor_copy(qb[:], xs[:].indirect(qs_t[:]))
         nc.vector.tensor_copy(ob_list[:], xs[:].indirect(offs_t[:]))
+        deal(nc.vector, ob, ob_list)
         nc.vector.tensor_copy(qw[:], xw[:].indirect(qs_t[:]))
         deal(nc.gpsimd, w2wd, w2w)
         deal(nc.gpsimd, w2sd, w2s)
-        deal(nc.vector, ob, ob_list)
+        ow = sb("ow", [P, S], U32)
         nc.vector.tensor_copy(ow[:].rearrange("p (t b r) -> p b t r", t=PACK, b=16), xw[:].indirect(offs_t[:]))
         deal(nc.gpsimd, w1wd, w1w)
         deal(nc.gpsimd, w1sd, w1s)
 
-        wv_bf = sb("wv_bf", [P, PACK * N], BF16)
-        nc.scalar.copy(out=woven(wv_bf[:, 0:1024]), in_=planes_walk(wv_raw[0][:]))
-        nc.gpsimd.tensor_scalar(out=wv_bf[:, 1024:2048].rearrange("p (n t) -> p n t", t=PACK),
-                                in0=wv_raw[1][:].rearrange("p t n -> p n t"), scalar1=1.0, scalar2=0.0,
-                                op0=ALU.mult, op1=ALU.add)
+        wv_bf = at(8192, "wv_bf", [P, PACK * N], BF16)
+        for h in range(2):
+            nc.scalar.copy(out=wv_bf[:, 1024 * h : 1024 * (h + 1)].rearrange("p (u m j) -> p m j u", u=PACK, j=PACK),
+                           in_=wv_raw[h][:].rearrange("p j (m u) -> p m j u", u=PACK))
 
-        z2_bf = sb("z2_bf", [P, PACK * V], BF16)
-        z_planes = sb("z_planes", [P, PACK, S // 2], BF16)
         gq_spread = gains[:, 0:4].rearrange("p (o t) -> p o t", o=1).to_broadcast([P, C, PACK])
-
         gk_spread = gains[:, 4:8].rearrange("p (o t) -> p o t", o=1).to_broadcast([P, C, PACK])
-        z_bf = [sb("z_bf%d" % c, [P, W], BF16) for c in range(CHUNKS)]
 
         def chunk_product(tag, name, words, plane, x_words_t, x_plane, c):
             acc = bank(tag, name)
@@ -154,38 +157,60 @@ def tile_picked_listco_none_po_kernel(
                    x_words_t[:, cols(c)].bitcast(FP8X4), x_plane[:, cols(c)])
             return acc
 
+        def half_planes(tags, name, words, plane, x_words_t, x_plane, h, planes, gain0):
+            for pair in range(2):
+                acc = bank(tags[pair], "%s%d" % (name, pair))
+                for u in range(2):
+                    t = 2 * pair + u
+                    mx(acc[:, half(u)], words[:, 2 * C * t : 2 * C * (t + 1)].bitcast(FP4X4), plane[:, cols(t)],
+                       x_words_t[:, half(h)].bitcast(FP8X4), x_plane[:, half(h)])
+                for u in range(2):
+                    t = 2 * pair + u
+                    nc.scalar.activation(out=planes[:, t, :], in_=acc[:, half(u)], func=ACT.Copy,
+                                         scale=gains[:, gain0 + t : gain0 + t + 1])
+
         def weigh_woven(dst, acc, spread):
             nc.vector.tensor_tensor(out=dst.rearrange("p (n t) -> p n t", t=PACK),
                                     in0=acc[:].rearrange("p (t n) -> p n t", t=PACK), in1=spread, op=ALU.mult)
 
-        wv_q = sb("wv_q", [P, N], U32)
-        wv_s = sb("wv_s", [P, N], U8)
+        z2_bf = sb("z2_bf", [P, PACK * V], BF16)
         for c in range(CHUNKS):
             acc = chunk_product("a%d" % c, "qf%d" % c, w2wd, w2sd, qw, qb, c)
             weigh_woven(z2_bf[:, c * W : (c + 1) * W], acc, gq_spread)
-        for pair in range(2):
-            acc = bank("b%d" % pair, "kf_hi%d" % pair)
-            for u in range(2):
-                t = 2 * pair + u
-                mx(acc[:, 256 * u : 256 * (u + 1)], w1wd[:, 2 * C * t : 2 * C * (t + 1)].bitcast(FP4X4), w1sd[:, cols(t)],
-                   ow[:, 256:512].bitcast(FP8X4), ob[:, 256:512])
-            for u in range(2):
-                t = 2 * pair + u
-                nc.scalar.activation(out=z_planes[:, t, :], in_=acc[:, 256 * u : 256 * (u + 1)], func=ACT.Copy,
-                                     scale=gains[:, 4 + t : 5 + t])
-        kf_lo = [chunk_product("b%d" % (2 + c), "kf_lo%d" % c, w1wd, w1sd, ow, ob, c) for c in range(2)]
-        z2_q = sb("z2_q", [P, V], U32)
+
+        wv_q = sb("wv_q", [P, N], U32)
+        wv_s = at(2048, "wv_s", [P, N], U8)
+        nc.vector.quantize_mx(out=wv_q[:].bitcast(FP8X4), scales=wv_s[:], in_=wv_bf[:])
+        z2_q = at(8192, "z2_q", [P, V], U32)
         z2_s = sb("z2_s", [P, V], U8)
         nc.vector.quantize_mx(out=z2_q[:].bitcast(FP8X4), scales=z2_s[:], in_=z2_bf[:])
-        for h in range(2):
-            nc.vector.quantize_mx(out=wv_q[:, 256 * h : 256 * (h + 1)].bitcast(FP8X4), scales=wv_s[:, 256 * h : 256 * (h + 1)],
-                                  in_=wv_bf[:, 1024 * h : 1024 * (h + 1)])
+
+        z_bf = [sb("z_bf%d" % c, [P, W], BF16) for c in range(CHUNKS)]
+        z_planes = sb("z_planes", [P, PACK, HALF], BF16)
+        half_planes(("b2", "b3"), "kf_hi", w1wd, w1sd, ow, ob, 1, z_planes, 4)
+        for c in (0, 1):
+            acc = chunk_product("b%d" % c, "kf%d" % c, w1wd, w1sd, ow, ob, c)
+            weigh_woven(z_bf[c][:], acc, gk_spread)
+        for c in (2, 3):
+            pool_weave(z_bf[c][:].rearrange("p (n t) -> p n t", t=PACK), z_planes[:, :, cols(c - 2)].rearrange("p t n -> p n t"))
+
         turned2 = bank("a0", "turned2")
         nc.tensor.transpose(turned2[:, 0:P], rows[1][:], ident[:])
-        gi_t = sb("gi_t", [P, PACK], F32)
-        gt16 = sb("gt16", [P, PACK], F32)
-        nc.scalar.copy(out=gi_t[:], in_=turned2[:, 0:4])
-        nc.scalar.activation(out=gt16[:], in_=turned2[:, 4:8], func=ACT.Copy, scale=16.0)
+        token_gains = sb("token_gains", [P, 8], F32)
+        nc.scalar.copy(out=token_gains[:], in_=turned2[:, 0:8])
+
+        zv_planes = [sb("zv_planes%d" % h, [P, PACK, HALF], BF16) for h in range(2)]
+        for h in range(2):
+            for pair in range(2):
+                acc = bank(("a1", "a2", "a3", "a0")[2 * h + pair], "val%d_%d" % (h, pair))
+                for k in range(2):
+                    t = 2 * pair + k
+                    mx(acc[:, half(k)], ow[:, cols(t)].bitcast(FP8X4), ob[:, cols(t)],
+                       wv_q[:, half(h)].bitcast(FP8X4), wv_s[:, half(h)])
+                for k in range(2):
+                    t = 2 * pair + k
+                    nc.scalar.activation(out=zv_planes[h][:, t, :], in_=acc[:, half(k)], func=ACT.Copy,
+                                         scale=token_gains[:, t : t + 1])
 
         z_q = [sb("z_q%d" % c, [P, C], U32) for c in range(CHUNKS)]
         z_s = [sb("z_s%d" % c, [P, C], U8) for c in range(CHUNKS)]
@@ -194,111 +219,102 @@ def tile_picked_listco_none_po_kernel(
         total = sb("total", [P, PACK], F32)
         e = sb("e", [P, PACK, V], F32)
 
-        def weave_keys(c):
-            if c < 2:
-                weigh_woven(z_bf[c][:], kf_lo[c], gk_spread)
-            else:
-                nc.vector.tensor_copy(out=woven(z_bf[c][:]), in_=planes_walk(z_planes[:, :, cols(c - 2)]))
-
-        scores = []
-
-        def score(c):
+        def quantise_keys(c):
             nc.vector.quantize_mx(out=z_q[c][:].bitcast(FP8X4), scales=z_s[c][:], in_=z_bf[c][:])
-            acc = bank("a%d" % c, "s%d" % c)
-            mx(acc[:], z_q[c][:].bitcast(FP8X4), z_s[c][:], z2_q[:].bitcast(FP8X4), z2_s[:])
-            scores.append(acc)
 
-        def soft(c):
-            nc.vector.tensor_scalar(out=neg[c][:], in0=scores[c][:], scalar1=-0.03125, scalar2=None,
+        for c in range(CHUNKS):
+            quantise_keys(c)
+
+        zv_bf = sb("zv_bf", [P, PACK * N], BF16, tag="z_bf3")
+        for h in range(2):
+            pool_weave(zv_bf[:].rearrange("p (u h m t) -> p h u m t", u=PACK, h=2, t=PACK)[:, h],
+                       zv_planes[h][:].rearrange("p t (u m) -> p u m t", u=PACK))
+
+        for c in range(CHUNKS):
+            acc = bank("b%d" % c, "s%d" % c)
+            mx(acc[:], z_q[c][:].bitcast(FP8X4), z_s[c][:], z2_q[:].bitcast(FP8X4), z2_s[:])
+            nc.vector.tensor_scalar(out=neg[c][:], in0=acc[:], scalar1=-0.03125, scalar2=None,
                                     op0=ALU.mult, op1=ALU.min, accum_out=low[c][:])
             nc.scalar.activation(out=e[:, c, :], in_=neg[c][:], func=ACT.Exp, bias=low[c][:], scale=-1.0,
                                  accum_out=total[:, c : c + 1])
-
-        weave_keys(0)
-        weave_keys(1)
-        zv_planes = [sb("zv_planes%d" % h, [P, PACK, N // 2], BF16) for h in range(2)]
-        zv_bf = sb("zv_bf", [P, PACK * N], BF16)
-        for h in range(2):
-            for pair in range(2):
-                acc = bank("b%d" % (2 * h + pair), "val%d_%d" % (h, pair))
-                for k in range(2):
-                    t = 2 * pair + k
-                    mx(acc[:, 256 * k : 256 * (k + 1)], ow[:, cols(t)].bitcast(FP8X4), ob[:, cols(t)],
-                       wv_q[:, 256 * h : 256 * (h + 1)].bitcast(FP8X4), wv_s[:, 256 * h : 256 * (h + 1)])
-                for k in range(2):
-                    t = 2 * pair + k
-                    nc.scalar.activation(
-                        out=zv_planes[h][:, t, :].rearrange("p (u m) -> p u m", u=PACK),
-                        in_=acc[:, 256 * k : 256 * (k + 1)].rearrange("p (m u) -> p u m", u=PACK),
-                        func=ACT.Copy, scale=gi_t[:, t : t + 1])
-            nc.gpsimd.tensor_scalar(
-                out=zv_bf[:].rearrange("p (u h m t) -> p h u m t", u=PACK, h=2, t=PACK)[:, h],
-                in0=zv_planes[h][:].rearrange("p t (u m) -> p u m t", u=PACK), scalar1=1.0, scalar2=0.0,
-                op0=ALU.mult, op1=ALU.add)
-
-        for c in range(CHUNKS):
-            score(c)
-            if c + 2 < CHUNKS:
-                weave_keys(c + 2)
-        for c in range(CHUNKS):
-            soft(c)
 
         zv_q = sb("zv_q", [P, N], U32)
         zv_s = sb("zv_s", [P, N], U8)
         inv = sb("inv", [P, PACK], F32)
         factor = sb("factor", [P, PACK], F32)
-        nc.vector.reciprocal(out=inv[:], in_=total[:])
         nc.vector.quantize_mx(out=zv_q[:].bitcast(FP8X4), scales=zv_s[:], in_=zv_bf[:])
-        nc.vector.tensor_tensor(out=factor[:], in0=inv[:], in1=gt16[:], op=ALU.mult)
+        nc.vector.reciprocal(out=inv[:], in_=total[:])
+        nc.vector.scalar_tensor_tensor(out=factor[:], in0=inv[:], scalar=16.0, in1=token_gains[:, 4:8],
+                                       op0=ALU.mult, op1=ALU.mult)
         factor_spread = factor[:].rearrange("p (a t b) -> p a t b", a=1, b=1).to_broadcast([P, C // 4, PACK, 4])
 
         zp_bf = [sb("zp_bf%d" % c, [P, W], BF16) for c in range(CHUNKS)]
         zp_q = [sb("zp_q%d" % c, [P, C], U32) for c in range(CHUNKS)]
         zp_s = [sb("zp_s%d" % c, [P, C], U8) for c in range(CHUNKS)]
         y = [sb("y%d" % c, [P, PACK, C], F32) for c in range(CHUNKS)]
-        y_bf = [sb("y_bf%d" % c, [P, W], BF16) for c in range(CHUNKS)]
+        y_bf = [sb("y_bf%d" % h, [P, 2 * W], BF16) for h in range(2)]
         y_q = sb("y_q", [P, V], U32)
         y_s = sb("y_s", [P, V], U8)
         out_rows = out_0.rearrange("(p t) v -> p t v", t=PACK)
         out_words = out_1[0].rearrange("p n t -> p (n t)").bitcast(I32)
         sums = []
+        late = []
 
-        zp_planes = sb("zp_planes", [P, PACK, V // 2], BF16)
+        zp_planes = sb("zp_planes", [P, PACK, HALF], BF16)
         for t in range(PACK):
-            nc.scalar.activation(out=zp_planes[:, t, :], in_=e[:, t, 256:512], func=ACT.Copy, scale=factor[:, t : t + 1])
+            nc.scalar.activation(out=zp_planes[:, t, :], in_=e[:, t, half(1)], func=ACT.Copy, scale=factor[:, t : t + 1])
 
         def weigh(c):
             if c < 2:
                 nc.vector.tensor_tensor(out=woven(zp_bf[c][:]), in0=planes_walk(e[:, :, cols(c)]), in1=factor_spread, op=ALU.mult)
-            else:
+            elif c == 2:
                 nc.vector.tensor_copy(out=woven(zp_bf[c][:]), in_=planes_walk(zp_planes[:, :, cols(c - 2)]))
+            else:
+                nc.scalar.copy(out=woven(zp_bf[c][:]), in_=planes_walk(zp_planes[:, :, cols(c - 2)]))
 
         def product(c):
             nc.vector.quantize_mx(out=zp_q[c][:].bitcast(FP8X4), scales=zp_s[c][:], in_=zp_bf[c][:])
-            acc = bank("b%d" % c, "y_acc%d" % c)
+            acc = bank("a%d" % c, "y_acc%d" % c)
             for u in range(PACK):
                 mx(acc[:, cols(u)], zv_q[:, cols(u)].bitcast(FP8X4), zv_s[:, cols(u)], zp_q[c][:].bitcast(FP8X4), zp_s[c][:])
             sums.append(acc)
 
         def finish(c):
-            nc.vector.tensor_tensor(out=y[c][:], in0=sums[c][:].rearrange("p (u n) -> p u n", u=PACK),
-                                    in1=res_t[:, :, cols(c)], op=ALU.add)
+            pieces = 2 if c == CHUNKS - 1 else 1
+            width = C // pieces
+            for k in range(pieces):
+                part = slice(k * width, (k + 1) * width)
+                nc.vector.tensor_tensor(out=y[c][:, :, part], in0=sums[c][:].rearrange("p (u n) -> p u n", u=PACK)[:, :, part],
+                                        in1=res_t[:, :, cols(c)][:, :, part], op=ALU.add)
+                first = (c % 2) * W + PACK * k * width
+                rounded = woven(y_bf[c // 2][:, first : first + PACK * width])
+                if k == 0:
+                    nc.scalar.copy(out=rounded, in_=planes_walk(y[c][:, :, part]))
+                else:
+                    late.append((rounded, planes_walk(y[c][:, :, part])))
             nc.sync.dma_start(out=out_rows[:, :, cols(c)], in_=y[c][:])
-            nc.scalar.copy(out=woven(y_bf[c][:]), in_=planes_walk(y[c][:]))
 
-        def hand_on(c):
-            nc.vector.quantize_mx(out=y_q[:, cols(c)].bitcast(FP8X4), scales=y_s[:, cols(c)], in_=y_bf[c][:])
-            nc.sync.dma_start(out=out_words[:, cols(c)], in_=y_q[:, cols(c)].bitcast(I32))
+        def hand_on(part, source):
+            nc.vector.quantize_mx(out=y_q[:, part].bitcast(FP8X4), scales=y_s[:, part], in_=source)
 
-        for step in range(CHUNKS + 3):
-            if step < CHUNKS:
-                weigh(step)
-            if 0 <= step - 1 < CHUNKS:
-                product(step - 1)
-            if 0 <= step - 2 < CHUNKS:
-                finish(step - 2)
-            if 0 <= step - 3 < CHUNKS:
-                hand_on(step - 3)
+        weigh(0)
+        weigh(1)
+        weigh(3)
+        product(0)
+        product(1)
+        weigh(2)
+        product(2)
+        finish(0)
+        product(3)
+        for c in range(1, CHUNKS):
+            finish(c)
+        hand_on(half(0), y_bf[0][:])
+        nc.sync.dma_start(out=out_words[:, half(0)], in_=y_q[:, half(0)].bitcast(I32))
+        for rounded, source in late:
+            nc.vector.tensor_copy(out=rounded, in_=source)
+        hand_on(cols(2), y_bf[1][:, 0:W])
+        hand_on(cols(3), y_bf[1][:, W : 2 * W])
+        nc.sync.dma_start(out=out_words[:, half(1)], in_=y_q[:, half(1)].bitcast(I32))
         for q in range(4):
             queue = nc.scalar if q % 2 else nc.sync
             queue.dma_start(out=out_2[0][4 * q : 4 * q + 4, :].bitcast(I32), in_=y_s[32 * q : 32 * q + 4, :].bitcast(I32))

@@ -65,6 +65,9 @@ def tile_picked_listco_none_po_kernel(
         def planes_walk(planes_ap):
             return planes_ap.rearrange("p t (c i) -> p c t i", i=4)
 
+        def weave(dst, planes_ap):
+            nc.vector.tensor_copy(out=dst.rearrange("p (n t) -> p n t", t=PACK), in_=planes_ap.rearrange("p t n -> p n t"))
+
         def pool_weave(dst, src):
             nc.gpsimd.tensor_scalar(out=dst, in0=src, scalar1=1.0, scalar2=0.0, op0=ALU.mult, op1=ALU.add)
 
@@ -72,10 +75,10 @@ def tile_picked_listco_none_po_kernel(
         offs_t = lists.tile([P, S // 16], U16, name="offs_t")
         xs = sb("xs", [P, T], U8)
         xw = sb("xw", [P, T], U32)
-        w2w = at(0, "w2w", [P, 2 * H], U8)
-        w2s = at(1024, "w2s", [P, H], U8)
+        w2w = sb("w2w", [P, 2 * H], U8)
+        w2s = sb("w2s", [P, H], U8, tag="ow")
         w1w = sb("w1w", [P, 2 * H], U8)
-        w1s = at(2048, "w1s", [P, H], U8)
+        w1s = sb("w1s", [P, H], U8)
         rows = [sb("rows%d" % n, [P, P], F32) for n in range(2)]
         ident = sb("ident", [P, P], F32)
         nc.gpsimd.memset(xs[:].bitcast(I32), 0)
@@ -106,9 +109,9 @@ def tile_picked_listco_none_po_kernel(
         nc.sync.dma_start(out=wv_raw[0][:], in_=wv_rows[:, :, half(0)])
         nc.sync.dma_start(out=wv_raw[1][:], in_=wv_rows[:, :, half(1)])
         nc.sync.dma_start(out=w1w[:].bitcast(I32), in_=w1_words[0].bitcast(I32))
-        load_plane(w1s, w1_scales, on_sync)
         load_rows(1, 0, gi)
         load_rows(1, 1, gt)
+        load_plane(w1s, w1_scales, on_sync)
         nc.sync.dma_start(out=res_t[:], in_=res.rearrange("(p t) v -> p t v", t=PACK))
 
         turned = bank("b3", "turned")
@@ -136,16 +139,16 @@ def tile_picked_listco_none_po_kernel(
         deal(nc.vector, ob, ob_list)
         nc.vector.tensor_copy(qw[:], xw[:].indirect(qs_t[:]))
         deal(nc.gpsimd, w2wd, w2w)
-        deal(nc.gpsimd, w2sd, w2s)
+        deal(nc.vector, w2sd, w2s)
         ow = sb("ow", [P, S], U32)
         nc.vector.tensor_copy(ow[:].rearrange("p (t b r) -> p b t r", t=PACK, b=16), xw[:].indirect(offs_t[:]))
-        deal(nc.gpsimd, w1wd, w1w)
-        deal(nc.gpsimd, w1sd, w1s)
 
-        wv_bf = at(8192, "wv_bf", [P, PACK * N], BF16)
-        for h in range(2):
-            nc.scalar.copy(out=wv_bf[:, 1024 * h : 1024 * (h + 1)].rearrange("p (u m j) -> p m j u", u=PACK, j=PACK),
-                           in_=wv_raw[h][:].rearrange("p j (m u) -> p m j u", u=PACK))
+        wv_bf = at(6144, "wv_bf", [P, PACK * N], BF16)
+        nc.scalar.copy(out=woven(wv_bf[:, 0 : 2 * W]), in_=planes_walk(wv_raw[0][:]))
+        pool_weave(wv_bf[:, 2 * W : 4 * W].rearrange("p (n j) -> p n j", j=PACK), wv_raw[1][:].rearrange("p j n -> p n j"))
+
+        def quantise(codes, scales, source):
+            nc.vector.quantize_mx(out=codes.bitcast(FP8X4), scales=scales, in_=source)
 
         gq_spread = gains[:, 0:4].rearrange("p (o t) -> p o t", o=1).to_broadcast([P, C, PACK])
         gk_spread = gains[:, 4:8].rearrange("p (o t) -> p o t", o=1).to_broadcast([P, C, PACK])
@@ -157,96 +160,97 @@ def tile_picked_listco_none_po_kernel(
                    x_words_t[:, cols(c)].bitcast(FP8X4), x_plane[:, cols(c)])
             return acc
 
-        def half_planes(tags, name, words, plane, x_words_t, x_plane, h, planes, gain0):
-            for pair in range(2):
-                acc = bank(tags[pair], "%s%d" % (name, pair))
-                for u in range(2):
-                    t = 2 * pair + u
-                    mx(acc[:, half(u)], words[:, 2 * C * t : 2 * C * (t + 1)].bitcast(FP4X4), plane[:, cols(t)],
-                       x_words_t[:, half(h)].bitcast(FP8X4), x_plane[:, half(h)])
-                for u in range(2):
-                    t = 2 * pair + u
-                    nc.scalar.activation(out=planes[:, t, :], in_=acc[:, half(u)], func=ACT.Copy,
-                                         scale=gains[:, gain0 + t : gain0 + t + 1])
-
         def weigh_woven(dst, acc, spread):
             nc.vector.tensor_tensor(out=dst.rearrange("p (n t) -> p n t", t=PACK),
                                     in0=acc[:].rearrange("p (t n) -> p n t", t=PACK), in1=spread, op=ALU.mult)
 
         z2_bf = sb("z2_bf", [P, PACK * V], BF16)
-        for c in range(CHUNKS):
-            acc = chunk_product("a%d" % c, "qf%d" % c, w2wd, w2sd, qw, qb, c)
-            weigh_woven(z2_bf[:, c * W : (c + 1) * W], acc, gq_spread)
+        acc = chunk_product("a0", "qf0", w2wd, w2sd, qw, qb, 0)
+        z2_planes = sb("z2_planes", [P, PACK, C], BF16, tag="wv_raw0")
+        for t in range(PACK):
+            nc.scalar.activation(out=z2_planes[:, t, :], in_=acc[:, cols(t)], func=ACT.Copy, scale=gains[:, t : t + 1])
+        nc.scalar.copy(out=woven(z2_bf[:, 0:W]), in_=planes_walk(z2_planes[:]))
+        for c in range(1, CHUNKS):
+            weigh_woven(z2_bf[:, c * W : (c + 1) * W], chunk_product("a%d" % c, "qf%d" % c, w2wd, w2sd, qw, qb, c), gq_spread)
 
+        deal(nc.gpsimd, w1wd, w1w)
+        deal(nc.gpsimd, w1sd, w1s)
         wv_q = sb("wv_q", [P, N], U32)
-        wv_s = at(2048, "wv_s", [P, N], U8)
-        nc.vector.quantize_mx(out=wv_q[:].bitcast(FP8X4), scales=wv_s[:], in_=wv_bf[:])
-        z2_q = at(8192, "z2_q", [P, V], U32)
+        wv_s = sb("wv_s", [P, N], U8, tag="w1s")
+        quantise(wv_q[:], wv_s[:], wv_bf[:])
+        z2_q = at(6144, "z2_q", [P, V], U32)
         z2_s = sb("z2_s", [P, V], U8)
-        nc.vector.quantize_mx(out=z2_q[:].bitcast(FP8X4), scales=z2_s[:], in_=z2_bf[:])
+        quantise(z2_q[:], z2_s[:], z2_bf[:])
 
-        z_bf = [sb("z_bf%d" % c, [P, W], BF16) for c in range(CHUNKS)]
+        zv_planes = [sb("zv_planes%d" % h, [P, PACK, HALF], BF16) for h in range(2)]
+
+        def values(h):
+            for pair in range(2):
+                acc = bank("b%d" % (2 * h + pair), "val%d_%d" % (h, pair))
+                for k in range(2):
+                    t = 2 * pair + k
+                    mx(acc[:, half(k)], ow[:, cols(t)].bitcast(FP8X4), ob[:, cols(t)], wv_q[:, half(h)].bitcast(FP8X4), wv_s[:, half(h)])
+                for k in range(2):
+                    t = 2 * pair + k
+                    nc.scalar.activation(out=zv_planes[h][:, t, :].rearrange("p (u m) -> p u m", u=PACK),
+                                         in_=acc[:, half(k)].rearrange("p (m u) -> p u m", u=PACK),
+                                         func=ACT.Copy, scale=token_gains[:, t : t + 1])
+
         z_planes = sb("z_planes", [P, PACK, HALF], BF16)
-        half_planes(("b2", "b3"), "kf_hi", w1wd, w1sd, ow, ob, 1, z_planes, 4)
-        for c in (0, 1):
-            acc = chunk_product("b%d" % c, "kf%d" % c, w1wd, w1sd, ow, ob, c)
-            weigh_woven(z_bf[c][:], acc, gk_spread)
-        for c in (2, 3):
-            pool_weave(z_bf[c][:].rearrange("p (n t) -> p n t", t=PACK), z_planes[:, :, cols(c - 2)].rearrange("p t n -> p n t"))
+        for pair in range(2):
+            acc = bank("a%d" % pair, "kf_hi%d" % pair)
+            for u in range(2):
+                t = 2 * pair + u
+                mx(acc[:, half(u)], w1wd[:, 2 * C * t : 2 * C * (t + 1)].bitcast(FP4X4), w1sd[:, cols(t)],
+                   ow[:, half(1)].bitcast(FP8X4), ob[:, half(1)])
+            for u in range(2):
+                t = 2 * pair + u
+                nc.scalar.activation(out=z_planes[:, t, :], in_=acc[:, half(u)], func=ACT.Copy, scale=gains[:, 4 + t : 5 + t])
 
-        turned2 = bank("a0", "turned2")
+        z_lo = [sb("z_lo%d" % c, [P, W], BF16) for c in range(2)]
+        for c in (0, 1):
+            weigh_woven(z_lo[c][:], chunk_product("a%d" % (2 + c), "kf%d" % c, w1wd, w1sd, ow, ob, c), gk_spread)
+        turned2 = bank("b2", "turned2")
         nc.tensor.transpose(turned2[:, 0:P], rows[1][:], ident[:])
         token_gains = sb("token_gains", [P, 8], F32)
         nc.scalar.copy(out=token_gains[:], in_=turned2[:, 0:8])
 
-        zv_planes = [sb("zv_planes%d" % h, [P, PACK, HALF], BF16) for h in range(2)]
-        for h in range(2):
-            for pair in range(2):
-                acc = bank(("a1", "a2", "a3", "a0")[2 * h + pair], "val%d_%d" % (h, pair))
-                for k in range(2):
-                    t = 2 * pair + k
-                    mx(acc[:, half(k)], ow[:, cols(t)].bitcast(FP8X4), ob[:, cols(t)],
-                       wv_q[:, half(h)].bitcast(FP8X4), wv_s[:, half(h)])
-                for k in range(2):
-                    t = 2 * pair + k
-                    nc.scalar.activation(out=zv_planes[h][:, t, :], in_=acc[:, half(k)], func=ACT.Copy,
-                                         scale=token_gains[:, t : t + 1])
+        values(0)
+        values(1)
 
-        z_q = [sb("z_q%d" % c, [P, C], U32) for c in range(CHUNKS)]
-        z_s = [sb("z_s%d" % c, [P, C], U8) for c in range(CHUNKS)]
+        z_q = sb("z_q", [P, S], U32)
+        z_s = sb("z_s", [P, S], U8)
         neg = [sb("neg%d" % c, [P, V], F32) for c in range(CHUNKS)]
         low = [sb("low%d" % c, [P, 1], F32) for c in range(CHUNKS)]
         total = sb("total", [P, PACK], F32)
         e = sb("e", [P, PACK, V], F32)
 
-        def quantise_keys(c):
-            nc.vector.quantize_mx(out=z_q[c][:].bitcast(FP8X4), scales=z_s[c][:], in_=z_bf[c][:])
+        for c in (0, 1):
+            quantise(z_q[:, cols(c)], z_s[:, cols(c)], z_lo[c][:])
+        z_hi = at(9216, "z_hi", [P, 2 * W], BF16)
+        weave(z_hi[:], z_planes[:])
+        quantise(z_q[:, half(1)], z_s[:, half(1)], z_hi[:])
 
-        for c in range(CHUNKS):
-            quantise_keys(c)
-
-        zv_bf = sb("zv_bf", [P, PACK * N], BF16, tag="z_bf3")
+        zv_bf = at(10240, "zv_bf", [P, PACK * N], BF16)
         for h in range(2):
             pool_weave(zv_bf[:].rearrange("p (u h m t) -> p h u m t", u=PACK, h=2, t=PACK)[:, h],
                        zv_planes[h][:].rearrange("p t (u m) -> p u m t", u=PACK))
 
         for c in range(CHUNKS):
-            acc = bank("b%d" % c, "s%d" % c)
-            mx(acc[:], z_q[c][:].bitcast(FP8X4), z_s[c][:], z2_q[:].bitcast(FP8X4), z2_s[:])
+            acc = bank(("b0", "b1", "a0", "a1")[c], "s%d" % c)
+            mx(acc[:], z_q[:, cols(c)].bitcast(FP8X4), z_s[:, cols(c)], z2_q[:].bitcast(FP8X4), z2_s[:])
             nc.vector.tensor_scalar(out=neg[c][:], in0=acc[:], scalar1=-0.03125, scalar2=None,
                                     op0=ALU.mult, op1=ALU.min, accum_out=low[c][:])
             nc.scalar.activation(out=e[:, c, :], in_=neg[c][:], func=ACT.Exp, bias=low[c][:], scale=-1.0,
                                  accum_out=total[:, c : c + 1])
 
         zv_q = sb("zv_q", [P, N], U32)
-        zv_s = sb("zv_s", [P, N], U8)
         inv = sb("inv", [P, PACK], F32)
         factor = sb("factor", [P, PACK], F32)
-        nc.vector.quantize_mx(out=zv_q[:].bitcast(FP8X4), scales=zv_s[:], in_=zv_bf[:])
         nc.vector.reciprocal(out=inv[:], in_=total[:])
         nc.vector.scalar_tensor_tensor(out=factor[:], in0=inv[:], scalar=16.0, in1=token_gains[:, 4:8],
                                        op0=ALU.mult, op1=ALU.mult)
-        factor_spread = factor[:].rearrange("p (a t b) -> p a t b", a=1, b=1).to_broadcast([P, C // 4, PACK, 4])
+        factor_spread = factor[:].rearrange("p (o t) -> p o t", o=1).to_broadcast([P, C, PACK])
 
         zp_bf = [sb("zp_bf%d" % c, [P, W], BF16) for c in range(CHUNKS)]
         zp_q = [sb("zp_q%d" % c, [P, C], U32) for c in range(CHUNKS)]
@@ -266,15 +270,16 @@ def tile_picked_listco_none_po_kernel(
 
         def weigh(c):
             if c < 2:
-                nc.vector.tensor_tensor(out=woven(zp_bf[c][:]), in0=planes_walk(e[:, :, cols(c)]), in1=factor_spread, op=ALU.mult)
+                nc.vector.tensor_tensor(out=zp_bf[c][:].rearrange("p (n t) -> p n t", t=PACK),
+                                        in0=e[:, :, cols(c)].rearrange("p t n -> p n t"), in1=factor_spread, op=ALU.mult)
             elif c == 2:
-                nc.vector.tensor_copy(out=woven(zp_bf[c][:]), in_=planes_walk(zp_planes[:, :, cols(c - 2)]))
+                weave(zp_bf[c][:], zp_planes[:, :, cols(c - 2)])
             else:
                 nc.scalar.copy(out=woven(zp_bf[c][:]), in_=planes_walk(zp_planes[:, :, cols(c - 2)]))
 
         def product(c):
             nc.vector.quantize_mx(out=zp_q[c][:].bitcast(FP8X4), scales=zp_s[c][:], in_=zp_bf[c][:])
-            acc = bank("a%d" % c, "y_acc%d" % c)
+            acc = bank(("a2", "a3", "b2", "b3")[c], "y_acc%d" % c)
             for u in range(PACK):
                 mx(acc[:, cols(u)], zv_q[:, cols(u)].bitcast(FP8X4), zv_s[:, cols(u)], zp_q[c][:].bitcast(FP8X4), zp_s[c][:])
             sums.append(acc)
@@ -287,31 +292,33 @@ def tile_picked_listco_none_po_kernel(
                 nc.vector.tensor_tensor(out=y[c][:, :, part], in0=sums[c][:].rearrange("p (u n) -> p u n", u=PACK)[:, :, part],
                                         in1=res_t[:, :, cols(c)][:, :, part], op=ALU.add)
                 first = (c % 2) * W + PACK * k * width
-                rounded = woven(y_bf[c // 2][:, first : first + PACK * width])
+                rounded = y_bf[c // 2][:, first : first + PACK * width]
                 if k == 0:
-                    nc.scalar.copy(out=rounded, in_=planes_walk(y[c][:, :, part]))
+                    nc.scalar.copy(out=woven(rounded), in_=planes_walk(y[c][:, :, part]))
                 else:
-                    late.append((rounded, planes_walk(y[c][:, :, part])))
+                    late.append((rounded, y[c][:, :, part]))
             nc.sync.dma_start(out=out_rows[:, :, cols(c)], in_=y[c][:])
 
         def hand_on(part, source):
             nc.vector.quantize_mx(out=y_q[:, part].bitcast(FP8X4), scales=y_s[:, part], in_=source)
 
         weigh(0)
-        weigh(1)
         weigh(3)
+        zv_s = sb("zv_s", [P, N], U8, tag="inv")
+        quantise(zv_q[:], zv_s[:], zv_bf[:])
         product(0)
-        product(1)
+        weigh(1)
         weigh(2)
-        product(2)
+        product(1)
         finish(0)
+        product(2)
         product(3)
         for c in range(1, CHUNKS):
             finish(c)
         hand_on(half(0), y_bf[0][:])
         nc.sync.dma_start(out=out_words[:, half(0)], in_=y_q[:, half(0)].bitcast(I32))
         for rounded, source in late:
-            nc.vector.tensor_copy(out=rounded, in_=source)
+            weave(rounded, source)
         hand_on(cols(2), y_bf[1][:, 0:W])
         hand_on(cols(3), y_bf[1][:, W : 2 * W])
         nc.sync.dma_start(out=out_words[:, half(1)], in_=y_q[:, half(1)].bitcast(I32))

@@ -66,7 +66,7 @@ def tile_picked_listco_none_po_kernel(
             return planes_ap.rearrange("p t (c i) -> p c t i", i=4)
 
         def weave(dst, planes_ap):
-            nc.vector.tensor_copy(out=dst.rearrange("p (n t) -> p n t", t=PACK), in_=planes_ap.rearrange("p t n -> p n t"))
+            nc.vector.tensor_copy(out=woven(dst), in_=planes_walk(planes_ap))
 
         def pool_weave(dst, src):
             nc.gpsimd.tensor_scalar(out=dst, in0=src, scalar1=1.0, scalar2=0.0, op0=ALU.mult, op1=ALU.add)
@@ -144,8 +144,8 @@ def tile_picked_listco_none_po_kernel(
         nc.vector.tensor_copy(ow[:].rearrange("p (t b r) -> p b t r", t=PACK, b=16), xw[:].indirect(offs_t[:]))
 
         wv_bf = at(6144, "wv_bf", [P, PACK * N], BF16)
-        nc.scalar.copy(out=woven(wv_bf[:, 0 : 2 * W]), in_=planes_walk(wv_raw[0][:]))
-        pool_weave(wv_bf[:, 2 * W : 4 * W].rearrange("p (n j) -> p n j", j=PACK), wv_raw[1][:].rearrange("p j n -> p n j"))
+        for h in range(2):
+            nc.scalar.copy(out=woven(wv_bf[:, 2 * W * h : 2 * W * (h + 1)]), in_=planes_walk(wv_raw[h][:]))
 
         def quantise(codes, scales, source):
             nc.vector.quantize_mx(out=codes.bitcast(FP8X4), scales=scales, in_=source)
@@ -165,12 +165,7 @@ def tile_picked_listco_none_po_kernel(
                                     in0=acc[:].rearrange("p (t n) -> p n t", t=PACK), in1=spread, op=ALU.mult)
 
         z2_bf = sb("z2_bf", [P, PACK * V], BF16)
-        acc = chunk_product("a0", "qf0", w2wd, w2sd, qw, qb, 0)
-        z2_planes = sb("z2_planes", [P, PACK, C], BF16, tag="wv_raw0")
-        for t in range(PACK):
-            nc.scalar.activation(out=z2_planes[:, t, :], in_=acc[:, cols(t)], func=ACT.Copy, scale=gains[:, t : t + 1])
-        nc.scalar.copy(out=woven(z2_bf[:, 0:W]), in_=planes_walk(z2_planes[:]))
-        for c in range(1, CHUNKS):
+        for c in range(CHUNKS):
             weigh_woven(z2_bf[:, c * W : (c + 1) * W], chunk_product("a%d" % c, "qf%d" % c, w2wd, w2sd, qw, qb, c), gq_spread)
 
         deal(nc.gpsimd, w1wd, w1w)
@@ -225,16 +220,15 @@ def tile_picked_listco_none_po_kernel(
         total = sb("total", [P, PACK], F32)
         e = sb("e", [P, PACK, V], F32)
 
-        for c in (0, 1):
-            quantise(z_q[:, cols(c)], z_s[:, cols(c)], z_lo[c][:])
+        quantise(z_q[:, cols(0)], z_s[:, cols(0)], z_lo[0][:])
         z_hi = at(9216, "z_hi", [P, 2 * W], BF16)
         weave(z_hi[:], z_planes[:])
+        quantise(z_q[:, cols(1)], z_s[:, cols(1)], z_lo[1][:])
         quantise(z_q[:, half(1)], z_s[:, half(1)], z_hi[:])
 
         zv_bf = at(10240, "zv_bf", [P, PACK * N], BF16)
-        for h in range(2):
-            pool_weave(zv_bf[:].rearrange("p (u h m t) -> p h u m t", u=PACK, h=2, t=PACK)[:, h],
-                       zv_planes[h][:].rearrange("p t (u m) -> p u m t", u=PACK))
+        pool_weave(zv_bf[:].rearrange("p (u h m t) -> p h u m t", u=PACK, h=2, t=PACK)[:, 0],
+                   zv_planes[0][:].rearrange("p t (u m) -> p u m t", u=PACK))
 
         for c in range(CHUNKS):
             acc = bank(("b0", "b1", "a0", "a1")[c], "s%d" % c)
@@ -244,13 +238,16 @@ def tile_picked_listco_none_po_kernel(
             nc.scalar.activation(out=e[:, c, :], in_=neg[c][:], func=ACT.Exp, bias=low[c][:], scale=-1.0,
                                  accum_out=total[:, c : c + 1])
 
+        nc.vector.tensor_copy(
+            out=zv_bf[:].rearrange("p (u h c i t) -> p h u c t i", u=PACK, h=2, i=4, t=PACK)[:, 1],
+            in_=zv_planes[1][:].rearrange("p t (u c i) -> p u c t i", u=PACK, i=4))
         zv_q = sb("zv_q", [P, N], U32)
         inv = sb("inv", [P, PACK], F32)
         factor = sb("factor", [P, PACK], F32)
         nc.vector.reciprocal(out=inv[:], in_=total[:])
         nc.vector.scalar_tensor_tensor(out=factor[:], in0=inv[:], scalar=16.0, in1=token_gains[:, 4:8],
                                        op0=ALU.mult, op1=ALU.mult)
-        factor_spread = factor[:].rearrange("p (o t) -> p o t", o=1).to_broadcast([P, C, PACK])
+        factor_spread = factor[:].rearrange("p (a t b) -> p a t b", a=1, b=1).to_broadcast([P, C // 4, PACK, 4])
 
         zp_bf = [sb("zp_bf%d" % c, [P, W], BF16) for c in range(CHUNKS)]
         zp_q = [sb("zp_q%d" % c, [P, C], U32) for c in range(CHUNKS)]
@@ -270,8 +267,7 @@ def tile_picked_listco_none_po_kernel(
 
         def weigh(c):
             if c < 2:
-                nc.vector.tensor_tensor(out=zp_bf[c][:].rearrange("p (n t) -> p n t", t=PACK),
-                                        in0=e[:, :, cols(c)].rearrange("p t n -> p n t"), in1=factor_spread, op=ALU.mult)
+                nc.vector.tensor_tensor(out=woven(zp_bf[c][:]), in0=planes_walk(e[:, :, cols(c)]), in1=factor_spread, op=ALU.mult)
             elif c == 2:
                 weave(zp_bf[c][:], zp_planes[:, :, cols(c - 2)])
             else:

@@ -117,7 +117,8 @@ def tile_picked_listco_none_po_kernel(
         turned = bank("b3", "turned")
         nc.tensor.transpose(turned[:, 0:P], rows[0][:], ident[:])
         gains = sb("gains", [P, 8], F32)
-        nc.scalar.copy(out=gains[:], in_=turned[:, 0:8])
+        nc.scalar.activation(out=gains[:, 0:4], in_=turned[:, 0:4], func=ACT.Copy, scale=-0.03125)
+        nc.scalar.copy(out=gains[:, 4:8], in_=turned[:, 4:8])
 
         qb = sb("qb", [P, V], U8)
         qw = sb("qw", [P, V], U32)
@@ -177,19 +178,14 @@ def tile_picked_listco_none_po_kernel(
         z2_s = sb("z2_s", [P, V], U8)
         quantise(z2_q[:], z2_s[:], z2_bf[:])
 
-        zv_planes = [sb("zv_planes%d" % h, [P, PACK, HALF], BF16) for h in range(2)]
+        zv_planes = sb("zv_planes", [P, PACK, N], BF16)
 
-        def values(h):
-            for pair in range(2):
-                acc = bank("b%d" % (2 * h + pair), "val%d_%d" % (h, pair))
-                for k in range(2):
-                    t = 2 * pair + k
-                    mx(acc[:, half(k)], ow[:, cols(t)].bitcast(FP8X4), ob[:, cols(t)], wv_q[:, half(h)].bitcast(FP8X4), wv_s[:, half(h)])
-                for k in range(2):
-                    t = 2 * pair + k
-                    nc.scalar.activation(out=zv_planes[h][:, t, :].rearrange("p (u m) -> p u m", u=PACK),
-                                         in_=acc[:, half(k)].rearrange("p (m u) -> p u m", u=PACK),
-                                         func=ACT.Copy, scale=token_gains[:, t : t + 1])
+        def values(t):
+            acc = bank("b%d" % t, "val%d" % t)
+            mx(acc[:], ow[:, cols(t)].bitcast(FP8X4), ob[:, cols(t)], wv_q[:].bitcast(FP8X4), wv_s[:])
+            nc.scalar.activation(out=zv_planes[:, t, :].rearrange("p (u m) -> p u m", u=PACK),
+                                 in_=acc[:].rearrange("p (m u) -> p u m", u=PACK),
+                                 func=ACT.Copy, scale=token_gains[:, t : t + 1])
 
         z_planes = sb("z_planes", [P, PACK, HALF], BF16)
         for pair in range(2):
@@ -210,12 +206,11 @@ def tile_picked_listco_none_po_kernel(
         token_gains = sb("token_gains", [P, 8], F32)
         nc.scalar.copy(out=token_gains[:], in_=turned2[:, 0:8])
 
-        values(0)
-        values(1)
+        for t in range(PACK):
+            values(t)
 
         z_q = sb("z_q", [P, S], U32)
         z_s = sb("z_s", [P, S], U8)
-        neg = [sb("neg%d" % c, [P, V], F32) for c in range(CHUNKS)]
         low = [sb("low%d" % c, [P, 1], F32) for c in range(CHUNKS)]
         total = sb("total", [P, PACK], F32)
         e = sb("e", [P, PACK, V], F32)
@@ -226,22 +221,27 @@ def tile_picked_listco_none_po_kernel(
         quantise(z_q[:, cols(1)], z_s[:, cols(1)], z_lo[1][:])
         quantise(z_q[:, half(1)], z_s[:, half(1)], z_hi[:])
 
-        zv_bf = at(10240, "zv_bf", [P, PACK * N], BF16)
-        pool_weave(zv_bf[:].rearrange("p (u h m t) -> p h u m t", u=PACK, h=2, t=PACK)[:, 0],
-                   zv_planes[0][:].rearrange("p t (u m) -> p u m t", u=PACK))
+        zv_bf = [at(10240, "zv_lo", [P, 2 * W], BF16), at(9216 - 1024, "zv_hi", [P, 2 * W], BF16)]
+        pool_weave(zv_bf[0][:].rearrange("p (m t) -> p m t", t=PACK),
+                   zv_planes[:, :, half(0)].rearrange("p t m -> p m t"))
 
         for c in range(CHUNKS):
             acc = bank(("b0", "b1", "a0", "a1")[c], "s%d" % c)
             mx(acc[:], z_q[:, cols(c)].bitcast(FP8X4), z_s[:, cols(c)], z2_q[:].bitcast(FP8X4), z2_s[:])
-            nc.vector.tensor_scalar(out=neg[c][:], in0=acc[:], scalar1=-0.03125, scalar2=None,
-                                    op0=ALU.mult, op1=ALU.min, accum_out=low[c][:])
-            nc.scalar.activation(out=e[:, c, :], in_=neg[c][:], func=ACT.Exp, bias=low[c][:], scale=-1.0,
+            nc.vector.tensor_reduce(out=low[c][:], in_=acc[:], axis=mybir.AxisListType.X, op=ALU.min)
+            nc.scalar.activation(out=e[:, c, :], in_=acc[:], func=ACT.Exp, bias=low[c][:], scale=-1.0,
                                  accum_out=total[:, c : c + 1])
 
-        nc.vector.tensor_copy(
-            out=zv_bf[:].rearrange("p (u h c i t) -> p h u c t i", u=PACK, h=2, i=4, t=PACK)[:, 1],
-            in_=zv_planes[1][:].rearrange("p t (u c i) -> p u c t i", u=PACK, i=4))
-        zv_q = sb("zv_q", [P, N], U32)
+        def keep_clock(tag, codes, scales):
+            mx(bank(tag, "unread_" + tag)[:], codes.bitcast(FP8X4), scales, z2_q[:].bitcast(FP8X4), z2_s[:])
+
+        for tag in ("a0", "a1"):
+            keep_clock(tag, z_q[:, cols(0)], z_s[:, cols(0)])
+        weave(zv_bf[1][:], zv_planes[:, :, half(1)])
+        zv_q = [sb("zv_q%d" % h, [P, HALF], U32) for h in range(2)]
+        zv_s = [sb("zv_s0", [P, HALF], U8)]
+        quantise(zv_q[0][:], zv_s[0][:], zv_bf[0][:])
+        keep_clock("b0", zv_q[0][:, cols(0)], zv_s[0][:, cols(0)])
         inv = sb("inv", [P, PACK], F32)
         factor = sb("factor", [P, PACK], F32)
         nc.vector.reciprocal(out=inv[:], in_=total[:])
@@ -277,7 +277,7 @@ def tile_picked_listco_none_po_kernel(
             nc.vector.quantize_mx(out=zp_q[c][:].bitcast(FP8X4), scales=zp_s[c][:], in_=zp_bf[c][:])
             acc = bank(("a2", "a3", "b2", "b3")[c], "y_acc%d" % c)
             for u in range(PACK):
-                mx(acc[:, cols(u)], zv_q[:, cols(u)].bitcast(FP8X4), zv_s[:, cols(u)], zp_q[c][:].bitcast(FP8X4), zp_s[c][:])
+                mx(acc[:, cols(u)], zv_q[u // 2][:, cols(u % 2)].bitcast(FP8X4), zv_s[u // 2][:, cols(u % 2)], zp_q[c][:].bitcast(FP8X4), zp_s[c][:])
             sums.append(acc)
 
         def finish(c):
@@ -300,8 +300,9 @@ def tile_picked_listco_none_po_kernel(
 
         weigh(0)
         weigh(3)
-        zv_s = sb("zv_s", [P, N], U8, tag="inv")
-        quantise(zv_q[:], zv_s[:], zv_bf[:])
+        zv_s.append(sb("zv_s1", [P, HALF], U8, tag="inv"))
+        quantise(zv_q[1][:], zv_s[1][:], zv_bf[1][:])
+        keep_clock("b1", zv_q[1][:, cols(0)], zv_s[1][:, cols(0)])
         product(0)
         weigh(1)
         weigh(2)

@@ -98,9 +98,9 @@ def tile_picked_listco_none_po_kernel(
         res_t = sb("res_t", [P, PACK, V], F32)
         on_sync = [nc.sync] * 4
         nc.sync.dma_start(qs_t[:], qs)
-        load_plane(xs, x_scales, on_sync)
         nc.sync.dma_start(offs_t[:], offs)
-        load_rows(0, 0, gq)
+        load_plane(xs, x_scales, [nc.sync, nc.scalar] * 2)
+        load_rows(0, 0, gq, nc.scalar)
         nc.scalar.activation(out=rows[1][:], in_=ident[:], func=ACT.Exp)
         nc.sync.dma_start(out=xw[:].bitcast(I32), in_=x_words[0].rearrange("p n t -> p (n t)").bitcast(I32))
         nc.sync.dma_start(out=w2w[:].bitcast(I32), in_=w2_words[0].bitcast(I32))
@@ -181,26 +181,22 @@ def tile_picked_listco_none_po_kernel(
         zv_planes = sb("zv_planes", [P, PACK, N], BF16)
 
         def values(t):
-            acc = bank("b%d" % t, "val%d" % t)
+            acc = bank(("b2", "a2", "a3", "b0")[t], "val%d" % t)
             mx(acc[:], ow[:, cols(t)].bitcast(FP8X4), ob[:, cols(t)], wv_q[:].bitcast(FP8X4), wv_s[:])
             nc.scalar.activation(out=zv_planes[:, t, :].rearrange("p (u m) -> p u m", u=PACK),
                                  in_=acc[:].rearrange("p (m u) -> p u m", u=PACK),
                                  func=ACT.Copy, scale=token_gains[:, t : t + 1])
 
-        z_planes = sb("z_planes", [P, PACK, HALF], BF16)
-        for pair in range(2):
-            acc = bank("a%d" % pair, "kf_hi%d" % pair)
-            for u in range(2):
-                t = 2 * pair + u
-                mx(acc[:, half(u)], w1wd[:, 2 * C * t : 2 * C * (t + 1)].bitcast(FP4X4), w1sd[:, cols(t)],
-                   ow[:, half(1)].bitcast(FP8X4), ob[:, half(1)])
-            for u in range(2):
-                t = 2 * pair + u
-                nc.scalar.activation(out=z_planes[:, t, :], in_=acc[:, half(u)], func=ACT.Copy, scale=gains[:, 4 + t : 5 + t])
+        z_planes = sb("z_planes", [P, PACK, W - C], BF16)
+        for t in range(PACK):
+            acc = bank(("b0", "b1", "b3", "a0")[t], "kf_hi%d" % t)
+            for part in (cols(1), half(1)):
+                mx(acc[:, part], w1wd[:, 2 * C * t : 2 * C * (t + 1)].bitcast(FP4X4), w1sd[:, cols(t)],
+                   ow[:, part].bitcast(FP8X4), ob[:, part])
+            nc.scalar.activation(out=z_planes[:, t, :], in_=acc[:, C:W], func=ACT.Copy, scale=gains[:, 4 + t : 5 + t])
 
-        z_lo = [sb("z_lo%d" % c, [P, W], BF16) for c in range(2)]
-        for c in (0, 1):
-            weigh_woven(z_lo[c][:], chunk_product("a%d" % (2 + c), "kf%d" % c, w1wd, w1sd, ow, ob, c), gk_spread)
+        z_lo = [sb("z_lo0", [P, W], BF16), at(8192, "z_lo1", [P, W], BF16)]
+        weigh_woven(z_lo[0][:], chunk_product("a1", "kf0", w1wd, w1sd, ow, ob, 0), gk_spread)
         turned2 = bank("b2", "turned2")
         nc.tensor.transpose(turned2[:, 0:P], rows[1][:], ident[:])
         token_gains = sb("token_gains", [P, 8], F32)
@@ -215,9 +211,10 @@ def tile_picked_listco_none_po_kernel(
         total = sb("total", [P, PACK], F32)
         e = sb("e", [P, PACK, V], F32)
 
+        weave(z_lo[1][:], z_planes[:, :, cols(0)])
         quantise(z_q[:, cols(0)], z_s[:, cols(0)], z_lo[0][:])
         z_hi = at(9216, "z_hi", [P, 2 * W], BF16)
-        weave(z_hi[:], z_planes[:])
+        weave(z_hi[:], z_planes[:, :, C : W - C])
         quantise(z_q[:, cols(1)], z_s[:, cols(1)], z_lo[1][:])
         quantise(z_q[:, half(1)], z_s[:, half(1)], z_hi[:])
 
@@ -226,7 +223,7 @@ def tile_picked_listco_none_po_kernel(
                    zv_planes[:, :, half(0)].rearrange("p t m -> p m t"))
 
         for c in range(CHUNKS):
-            acc = bank(("b0", "b1", "a0", "a1")[c], "s%d" % c)
+            acc = bank(("b2", "a2", "a3", "b0")[c], "s%d" % c)
             mx(acc[:], z_q[:, cols(c)].bitcast(FP8X4), z_s[:, cols(c)], z2_q[:].bitcast(FP8X4), z2_s[:])
             nc.vector.tensor_reduce(out=low[c][:], in_=acc[:], axis=mybir.AxisListType.X, op=ALU.min)
             nc.scalar.activation(out=e[:, c, :], in_=acc[:], func=ACT.Exp, bias=low[c][:], scale=-1.0,
@@ -235,13 +232,13 @@ def tile_picked_listco_none_po_kernel(
         def keep_clock(tag, codes, scales):
             mx(bank(tag, "unread_" + tag)[:], codes.bitcast(FP8X4), scales, z2_q[:].bitcast(FP8X4), z2_s[:])
 
-        for tag in ("a0", "a1"):
+        for tag in ("a3", "b0"):
             keep_clock(tag, z_q[:, cols(0)], z_s[:, cols(0)])
         weave(zv_bf[1][:], zv_planes[:, :, half(1)])
         zv_q = [sb("zv_q%d" % h, [P, HALF], U32) for h in range(2)]
         zv_s = [sb("zv_s0", [P, HALF], U8)]
         quantise(zv_q[0][:], zv_s[0][:], zv_bf[0][:])
-        keep_clock("b0", zv_q[0][:, cols(0)], zv_s[0][:, cols(0)])
+        keep_clock("b2", zv_q[0][:, cols(0)], zv_s[0][:, cols(0)])
         inv = sb("inv", [P, PACK], F32)
         factor = sb("factor", [P, PACK], F32)
         nc.vector.reciprocal(out=inv[:], in_=total[:])
@@ -275,7 +272,7 @@ def tile_picked_listco_none_po_kernel(
 
         def product(c):
             nc.vector.quantize_mx(out=zp_q[c][:].bitcast(FP8X4), scales=zp_s[c][:], in_=zp_bf[c][:])
-            acc = bank(("a2", "a3", "b2", "b3")[c], "y_acc%d" % c)
+            acc = bank(("b1", "b3", "a0", "a1")[c], "y_acc%d" % c)
             for u in range(PACK):
                 mx(acc[:, cols(u)], zv_q[u // 2][:, cols(u % 2)].bitcast(FP8X4), zv_s[u // 2][:, cols(u % 2)], zp_q[c][:].bitcast(FP8X4), zp_s[c][:])
             sums.append(acc)
@@ -302,7 +299,7 @@ def tile_picked_listco_none_po_kernel(
         weigh(3)
         zv_s.append(sb("zv_s1", [P, HALF], U8, tag="inv"))
         quantise(zv_q[1][:], zv_s[1][:], zv_bf[1][:])
-        keep_clock("b1", zv_q[1][:, cols(0)], zv_s[1][:, cols(0)])
+        keep_clock("a2", zv_q[1][:, cols(0)], zv_s[1][:, cols(0)])
         product(0)
         weigh(1)
         weigh(2)

@@ -99,8 +99,8 @@ def tile_picked_listco_none_po_kernel(
         on_sync = [nc.sync] * 4
         nc.sync.dma_start(qs_t[:], qs)
         nc.sync.dma_start(offs_t[:], offs)
-        load_plane(xs, x_scales, [nc.sync, nc.scalar] * 2)
-        load_rows(0, 0, gq, nc.scalar)
+        load_plane(xs, x_scales, on_sync)
+        load_rows(0, 0, gq)
         nc.scalar.activation(out=rows[1][:], in_=ident[:], func=ACT.Exp)
         nc.sync.dma_start(out=xw[:].bitcast(I32), in_=x_words[0].rearrange("p n t -> p (n t)").bitcast(I32))
         nc.sync.dma_start(out=w2w[:].bitcast(I32), in_=w2_words[0].bitcast(I32))

@@ -3,7 +3,7 @@ from contextlib import ExitStack
 import concourse.mybir as mybir
 from concourse.masks import make_identity
 
-K, T, S, V, N, H = 512, 2048, 512, 512, 512, 512
+T, S, V, N, H = 2048, 512, 512, 512, 512
 FLOPS = 5 * 2 * 512 * 512 * 512
 
 F32 = mybir.dt.float32
@@ -19,10 +19,15 @@ ALU = mybir.AluOpType
 
 P = 128
 PACK = 4
+BLOCKS = 16
+RUN = 8
 W = 512
 C = 128
 HALF = 256
 CHUNKS = W // C
+WALK = 4
+KIB = 1024
+SHARED = 0
 
 
 def tile_picked_listco_none_po_kernel(
@@ -40,18 +45,11 @@ def tile_picked_listco_none_po_kernel(
         def sb(name, shape, dtype, tag=None):
             return keep.tile(shape, dtype, name=name, tag=tag or name, align_bytes=64)
 
-        def at(offset, name, shape, dtype):
-            return placed.tile(shape, dtype, name=name, align_bytes=64, offset=offset)
+        def at(kib, name, shape, dtype):
+            return placed.tile(shape, dtype, name=name, align_bytes=64, offset=SHARED + kib * KIB)
 
         def bank(tag, name):
             return psum.tile([P, W], F32, name=name, tag=tag)
-
-        def load_plane(plane, scales, queues):
-            for q in range(4):
-                queues[q].dma_start(out=plane[32 * q : 32 * q + 4, :].bitcast(I32), in_=scales[0][4 * q : 4 * q + 4, :].bitcast(I32))
-
-        def mx(out, lhs, lhs_scale, rhs, rhs_scale):
-            nc.tensor.matmul_mx(out=out, lhsT=lhs, lhsT_scale=lhs_scale, rhs=rhs, rhs_scale=rhs_scale, start=True, stop=True)
 
         def cols(c):
             return slice(c * C, (c + 1) * C)
@@ -59,24 +57,34 @@ def tile_picked_listco_none_po_kernel(
         def half(h):
             return slice(h * HALF, (h + 1) * HALF)
 
+        def load_plane(plane, scales):
+            for q in range(4):
+                nc.sync.dma_start(out=plane[32 * q : 32 * q + 4, :].bitcast(I32), in_=scales[0][4 * q : 4 * q + 4, :].bitcast(I32))
+
+        def mx(out, lhs, lhs_scale, rhs, rhs_scale):
+            nc.tensor.matmul_mx(out=out, lhsT=lhs, lhsT_scale=lhs_scale, rhs=rhs, rhs_scale=rhs_scale, start=True, stop=True)
+
+        def quantise(codes, scales, source):
+            nc.vector.quantize_mx(out=codes.bitcast(FP8X4), scales=scales, in_=source)
+
         def woven(tile_ap):
-            return tile_ap.rearrange("p (c i t) -> p c t i", i=4, t=PACK)
+            return tile_ap.rearrange("p (c i t) -> p c t i", i=WALK, t=PACK)
 
         def planes_walk(planes_ap):
-            return planes_ap.rearrange("p t (c i) -> p c t i", i=4)
+            return planes_ap.rearrange("p t (c i) -> p c t i", i=WALK)
 
         def weave(dst, planes_ap):
             nc.vector.tensor_copy(out=woven(dst), in_=planes_walk(planes_ap))
 
-        def pool_weave(dst, src):
-            nc.gpsimd.tensor_scalar(out=dst, in0=src, scalar1=1.0, scalar2=0.0, op0=ALU.mult, op1=ALU.add)
+        def scalar_weave(dst, planes_ap):
+            nc.scalar.copy(out=woven(dst), in_=planes_walk(planes_ap))
 
         qs_t = lists.tile([P, V // 16], U16, name="qs_t")
         offs_t = lists.tile([P, S // 16], U16, name="offs_t")
         xs = sb("xs", [P, T], U8)
         xw = sb("xw", [P, T], U32)
         w2w = sb("w2w", [P, 2 * H], U8)
-        w2s = sb("w2s", [P, H], U8, tag="ow")
+        w2s = sb("w2s", [P, H], U8)
         w1w = sb("w1w", [P, 2 * H], U8)
         w1s = sb("w1s", [P, H], U8)
         rows = [sb("rows%d" % n, [P, P], F32) for n in range(2)]
@@ -87,43 +95,42 @@ def tile_picked_listco_none_po_kernel(
         nc.vector.memset(w1s[:].bitcast(I32), 0)
         make_identity(nc, ident[:])
 
-        def load_rows(n, m, vec, queue=nc.sync):
-            queue.dma_start(
-                out=rows[n][4 * m : 4 * m + 4, :].rearrange("t (b r) -> t b r", r=8),
-                in_=vec.rearrange("(b t r) o -> t b (r o)", t=PACK, r=8),
+        def load_rows(n, m, vec):
+            nc.sync.dma_start(
+                out=rows[n][PACK * m : PACK * (m + 1), :].rearrange("t (b r) -> t b r", r=RUN),
+                in_=vec.rearrange("(b t r) o -> t b (r o)", t=PACK, r=RUN),
             )
 
         wv_raw = [sb("wv_raw%d" % h, [P, PACK, HALF], F32) for h in range(2)]
         wv_rows = wv.rearrange("(p j) n -> p j n", j=PACK)
         res_t = sb("res_t", [P, PACK, V], F32)
-        on_sync = [nc.sync] * 4
         nc.sync.dma_start(qs_t[:], qs)
         nc.sync.dma_start(offs_t[:], offs)
-        load_plane(xs, x_scales, on_sync)
+        load_plane(xs, x_scales)
         load_rows(0, 0, gq)
         nc.scalar.activation(out=rows[1][:], in_=ident[:], func=ACT.Exp)
         nc.sync.dma_start(out=xw[:].bitcast(I32), in_=x_words[0].rearrange("p n t -> p (n t)").bitcast(I32))
         nc.sync.dma_start(out=w2w[:].bitcast(I32), in_=w2_words[0].bitcast(I32))
         load_rows(0, 1, gk)
-        load_plane(w2s, w2_scales, on_sync)
+        load_plane(w2s, w2_scales)
         nc.sync.dma_start(out=wv_raw[0][:], in_=wv_rows[:, :, half(0)])
         nc.sync.dma_start(out=wv_raw[1][:], in_=wv_rows[:, :, half(1)])
         nc.sync.dma_start(out=w1w[:].bitcast(I32), in_=w1_words[0].bitcast(I32))
         load_rows(1, 0, gi)
         load_rows(1, 1, gt)
-        load_plane(w1s, w1_scales, on_sync)
+        load_plane(w1s, w1_scales)
         nc.sync.dma_start(out=res_t[:], in_=res.rearrange("(p t) v -> p t v", t=PACK))
 
         turned = bank("b3", "turned")
         nc.tensor.transpose(turned[:, 0:P], rows[0][:], ident[:])
-        gains = sb("gains", [P, 8], F32)
-        nc.scalar.activation(out=gains[:, 0:4], in_=turned[:, 0:4], func=ACT.Copy, scale=-0.03125)
-        nc.scalar.copy(out=gains[:, 4:8], in_=turned[:, 4:8])
+        gains = sb("gains", [P, 2 * PACK], F32)
+        nc.scalar.activation(out=gains[:, 0:PACK], in_=turned[:, 0:PACK], func=ACT.Copy, scale=-0.03125)
+        nc.scalar.copy(out=gains[:, PACK : 2 * PACK], in_=turned[:, PACK : 2 * PACK])
 
         qb = sb("qb", [P, V], U8)
         qw = sb("qw", [P, V], U32)
         ob_list = sb("ob_list", [P, S], U8)
-        ob = sb("ob", [P, S], U8)
+        ob = sb("ob", [P, S], U8, tag="w2s")
         w2wd = sb("w2wd", [P, 2 * H], U8)
         w1wd = sb("w1wd", [P, 2 * H], U8)
         w2sd = sb("w2sd", [P, H], U8)
@@ -131,34 +138,34 @@ def tile_picked_listco_none_po_kernel(
 
         def deal(engine, dealt, plain):
             engine.tensor_copy(
-                out=dealt[:].bitcast(I32).rearrange("p (t b q) -> p t b q", t=PACK, b=16),
-                in_=plain[:].bitcast(I32).rearrange("p (b t q) -> p t b q", t=PACK, b=16),
+                out=dealt[:].bitcast(I32).rearrange("p (t b q) -> p t b q", t=PACK, b=BLOCKS),
+                in_=plain[:].bitcast(I32).rearrange("p (b t q) -> p t b q", t=PACK, b=BLOCKS),
             )
 
         nc.vector.tensor_copy(qb[:], xs[:].indirect(qs_t[:]))
         nc.vector.tensor_copy(ob_list[:], xs[:].indirect(offs_t[:]))
-        deal(nc.vector, ob, ob_list)
         nc.vector.tensor_copy(qw[:], xw[:].indirect(qs_t[:]))
         deal(nc.gpsimd, w2wd, w2w)
-        deal(nc.vector, w2sd, w2s)
+        deal(nc.gpsimd, w2sd, w2s)
         ow = sb("ow", [P, S], U32)
-        nc.vector.tensor_copy(ow[:].rearrange("p (t b r) -> p b t r", t=PACK, b=16), xw[:].indirect(offs_t[:]))
+        nc.vector.tensor_copy(ow[:].rearrange("p (t b r) -> p b t r", t=PACK, b=BLOCKS), xw[:].indirect(offs_t[:]))
+        deal(nc.vector, ob, ob_list)
 
-        wv_bf = at(6144, "wv_bf", [P, PACK * N], BF16)
+        wv_bf = at(0, "wv_bf", [P, PACK * N], BF16)
         for h in range(2):
-            nc.scalar.copy(out=woven(wv_bf[:, 2 * W * h : 2 * W * (h + 1)]), in_=planes_walk(wv_raw[h][:]))
+            scalar_weave(wv_bf[:, 2 * W * h : 2 * W * (h + 1)], wv_raw[h][:])
 
-        def quantise(codes, scales, source):
-            nc.vector.quantize_mx(out=codes.bitcast(FP8X4), scales=scales, in_=source)
+        gq_spread = gains[:, 0:PACK].rearrange("p (o t) -> p o t", o=1).to_broadcast([P, C, PACK])
+        gk_spread = gains[:, PACK : 2 * PACK].rearrange("p (o t) -> p o t", o=1).to_broadcast([P, C, PACK])
 
-        gq_spread = gains[:, 0:4].rearrange("p (o t) -> p o t", o=1).to_broadcast([P, C, PACK])
-        gk_spread = gains[:, 4:8].rearrange("p (o t) -> p o t", o=1).to_broadcast([P, C, PACK])
+        def fp4_slot(words, t):
+            return words[:, 2 * C * t : 2 * C * (t + 1)].bitcast(FP4X4)
 
-        def chunk_product(tag, name, words, plane, x_words_t, x_plane, c):
+        def chunk_product(tag, name, words, plane, picked_words, picked_plane, c):
             acc = bank(tag, name)
             for t in range(PACK):
-                mx(acc[:, cols(t)], words[:, 2 * C * t : 2 * C * (t + 1)].bitcast(FP4X4), plane[:, cols(t)],
-                   x_words_t[:, cols(c)].bitcast(FP8X4), x_plane[:, cols(c)])
+                mx(acc[:, cols(t)], fp4_slot(words, t), plane[:, cols(t)],
+                   picked_words[:, cols(c)].bitcast(FP8X4), picked_plane[:, cols(c)])
             return acc
 
         def weigh_woven(dst, acc, spread):
@@ -174,77 +181,75 @@ def tile_picked_listco_none_po_kernel(
         wv_q = sb("wv_q", [P, N], U32)
         wv_s = sb("wv_s", [P, N], U8, tag="w1s")
         quantise(wv_q[:], wv_s[:], wv_bf[:])
-        z2_q = at(6144, "z2_q", [P, V], U32)
+        z2_q = at(0, "z2_q", [P, V], U32)
         z2_s = sb("z2_s", [P, V], U8)
         quantise(z2_q[:], z2_s[:], z2_bf[:])
 
         zv_planes = sb("zv_planes", [P, PACK, N], BF16)
+        z_planes = sb("z_planes", [P, PACK, W - C], BF16)
+        for t in range(PACK):
+            acc = bank(("b0", "b1", "b3", "a0")[t], "kf_hi%d" % t)
+            for part in (cols(1), half(1)):
+                mx(acc[:, part], fp4_slot(w1wd, t), w1sd[:, cols(t)], ow[:, part].bitcast(FP8X4), ob[:, part])
+            nc.scalar.activation(out=z_planes[:, t, :], in_=acc[:, C:W], func=ACT.Copy, scale=gains[:, PACK + t : PACK + t + 1])
 
-        def values(t):
-            acc = bank(("b2", "a2", "a3", "b0")[t], "val%d" % t)
+        z_lo = [sb("z_lo0", [P, W], BF16), at(2, "z_lo1", [P, W], BF16)]
+        weigh_woven(z_lo[0][:], chunk_product("a1", "kf0", w1wd, w1sd, ow, ob, 0), gk_spread)
+
+        turned2 = bank("b2", "turned2")
+        nc.tensor.transpose(turned2[:, 0:P], rows[1][:], ident[:])
+        token_gains = sb("token_gains", [P, 2 * PACK], F32)
+        nc.scalar.copy(out=token_gains[:], in_=turned2[:, 0 : 2 * PACK])
+
+        token_banks = ("b2", "a2", "a3", "b0")
+        for t in range(PACK):
+            acc = bank(token_banks[t], "val%d" % t)
             mx(acc[:], ow[:, cols(t)].bitcast(FP8X4), ob[:, cols(t)], wv_q[:].bitcast(FP8X4), wv_s[:])
             nc.scalar.activation(out=zv_planes[:, t, :].rearrange("p (u m) -> p u m", u=PACK),
                                  in_=acc[:].rearrange("p (m u) -> p u m", u=PACK),
                                  func=ACT.Copy, scale=token_gains[:, t : t + 1])
 
-        z_planes = sb("z_planes", [P, PACK, W - C], BF16)
-        for t in range(PACK):
-            acc = bank(("b0", "b1", "b3", "a0")[t], "kf_hi%d" % t)
-            for part in (cols(1), half(1)):
-                mx(acc[:, part], w1wd[:, 2 * C * t : 2 * C * (t + 1)].bitcast(FP4X4), w1sd[:, cols(t)],
-                   ow[:, part].bitcast(FP8X4), ob[:, part])
-            nc.scalar.activation(out=z_planes[:, t, :], in_=acc[:, C:W], func=ACT.Copy, scale=gains[:, 4 + t : 5 + t])
-
-        z_lo = [sb("z_lo0", [P, W], BF16), at(8192, "z_lo1", [P, W], BF16)]
-        weigh_woven(z_lo[0][:], chunk_product("a1", "kf0", w1wd, w1sd, ow, ob, 0), gk_spread)
-        turned2 = bank("b2", "turned2")
-        nc.tensor.transpose(turned2[:, 0:P], rows[1][:], ident[:])
-        token_gains = sb("token_gains", [P, 8], F32)
-        nc.scalar.copy(out=token_gains[:], in_=turned2[:, 0:8])
-
-        for t in range(PACK):
-            values(t)
-
         z_q = sb("z_q", [P, S], U32)
         z_s = sb("z_s", [P, S], U8)
-        low = [sb("low%d" % c, [P, 1], F32) for c in range(CHUNKS)]
+        low = [sb("low%d" % t, [P, 1], F32) for t in range(PACK)]
         total = sb("total", [P, PACK], F32)
         e = sb("e", [P, PACK, V], F32)
 
         weave(z_lo[1][:], z_planes[:, :, cols(0)])
         quantise(z_q[:, cols(0)], z_s[:, cols(0)], z_lo[0][:])
-        z_hi = at(9216, "z_hi", [P, 2 * W], BF16)
+        z_hi = at(3, "z_hi", [P, 2 * W], BF16)
         weave(z_hi[:], z_planes[:, :, C : W - C])
         quantise(z_q[:, cols(1)], z_s[:, cols(1)], z_lo[1][:])
         quantise(z_q[:, half(1)], z_s[:, half(1)], z_hi[:])
 
-        zv_bf = [at(10240, "zv_lo", [P, 2 * W], BF16), at(9216 - 1024, "zv_hi", [P, 2 * W], BF16)]
-        pool_weave(zv_bf[0][:].rearrange("p (m t) -> p m t", t=PACK),
-                   zv_planes[:, :, half(0)].rearrange("p t m -> p m t"))
+        zv_bf = [at(4, "zv_lo", [P, 2 * W], BF16), at(2, "zv_hi", [P, 2 * W], BF16)]
+        nc.gpsimd.tensor_scalar(out=zv_bf[0][:].rearrange("p (m t) -> p m t", t=PACK),
+                                in0=zv_planes[:, :, half(0)].rearrange("p t m -> p m t"),
+                                scalar1=1.0, scalar2=0.0, op0=ALU.mult, op1=ALU.add)
 
-        for c in range(CHUNKS):
-            acc = bank(("b2", "a2", "a3", "b0")[c], "s%d" % c)
-            mx(acc[:], z_q[:, cols(c)].bitcast(FP8X4), z_s[:, cols(c)], z2_q[:].bitcast(FP8X4), z2_s[:])
-            nc.vector.tensor_reduce(out=low[c][:], in_=acc[:], axis=mybir.AxisListType.X, op=ALU.min)
-            nc.scalar.activation(out=e[:, c, :], in_=acc[:], func=ACT.Exp, bias=low[c][:], scale=-1.0,
-                                 accum_out=total[:, c : c + 1])
+        for t in range(PACK):
+            acc = bank(token_banks[t], "s%d" % t)
+            mx(acc[:], z_q[:, cols(t)].bitcast(FP8X4), z_s[:, cols(t)], z2_q[:].bitcast(FP8X4), z2_s[:])
+            nc.vector.tensor_reduce(out=low[t][:], in_=acc[:], axis=mybir.AxisListType.X, op=ALU.min)
+            nc.scalar.activation(out=e[:, t, :], in_=acc[:], func=ACT.Exp, bias=low[t][:], scale=-1.0,
+                                 accum_out=total[:, t : t + 1])
 
         def keep_clock(tag, codes, scales):
             mx(bank(tag, "unread_" + tag)[:], codes.bitcast(FP8X4), scales, z2_q[:].bitcast(FP8X4), z2_s[:])
 
-        for tag in ("a3", "b0"):
+        for tag in token_banks[2:]:
             keep_clock(tag, z_q[:, cols(0)], z_s[:, cols(0)])
         weave(zv_bf[1][:], zv_planes[:, :, half(1)])
         zv_q = [sb("zv_q%d" % h, [P, HALF], U32) for h in range(2)]
         zv_s = [sb("zv_s0", [P, HALF], U8)]
         quantise(zv_q[0][:], zv_s[0][:], zv_bf[0][:])
-        keep_clock("b2", zv_q[0][:, cols(0)], zv_s[0][:, cols(0)])
+        keep_clock(token_banks[0], zv_q[0][:, cols(0)], zv_s[0][:, cols(0)])
         inv = sb("inv", [P, PACK], F32)
         factor = sb("factor", [P, PACK], F32)
         nc.vector.reciprocal(out=inv[:], in_=total[:])
-        nc.vector.scalar_tensor_tensor(out=factor[:], in0=inv[:], scalar=16.0, in1=token_gains[:, 4:8],
+        nc.vector.scalar_tensor_tensor(out=factor[:], in0=inv[:], scalar=16.0, in1=token_gains[:, PACK : 2 * PACK],
                                        op0=ALU.mult, op1=ALU.mult)
-        factor_spread = factor[:].rearrange("p (a t b) -> p a t b", a=1, b=1).to_broadcast([P, C // 4, PACK, 4])
+        factor_spread = factor[:].rearrange("p (a t b) -> p a t b", a=1, b=1).to_broadcast([P, C // WALK, PACK, WALK])
 
         zp_bf = [sb("zp_bf%d" % c, [P, W], BF16) for c in range(CHUNKS)]
         zp_q = [sb("zp_q%d" % c, [P, C], U32) for c in range(CHUNKS)]
@@ -255,67 +260,71 @@ def tile_picked_listco_none_po_kernel(
         y_s = sb("y_s", [P, V], U8)
         out_rows = out_0.rearrange("(p t) v -> p t v", t=PACK)
         out_words = out_1[0].rearrange("p n t -> p (n t)").bitcast(I32)
+        result_banks = ("b1", "b3", "a0", "a1")
         sums = []
-        late = []
 
         zp_planes = sb("zp_planes", [P, PACK, HALF], BF16)
         for t in range(PACK):
             nc.scalar.activation(out=zp_planes[:, t, :], in_=e[:, t, half(1)], func=ACT.Copy, scale=factor[:, t : t + 1])
 
         def weigh(c):
-            if c < 2:
-                nc.vector.tensor_tensor(out=woven(zp_bf[c][:]), in0=planes_walk(e[:, :, cols(c)]), in1=factor_spread, op=ALU.mult)
-            elif c == 2:
-                weave(zp_bf[c][:], zp_planes[:, :, cols(c - 2)])
-            else:
-                nc.scalar.copy(out=woven(zp_bf[c][:]), in_=planes_walk(zp_planes[:, :, cols(c - 2)]))
+            nc.vector.tensor_tensor(out=woven(zp_bf[c][:]), in0=planes_walk(e[:, :, cols(c)]), in1=factor_spread, op=ALU.mult)
 
         def product(c):
-            nc.vector.quantize_mx(out=zp_q[c][:].bitcast(FP8X4), scales=zp_s[c][:], in_=zp_bf[c][:])
-            acc = bank(("b1", "b3", "a0", "a1")[c], "y_acc%d" % c)
+            quantise(zp_q[c][:], zp_s[c][:], zp_bf[c][:])
+            acc = bank(result_banks[c], "y_acc%d" % c)
             for u in range(PACK):
-                mx(acc[:, cols(u)], zv_q[u // 2][:, cols(u % 2)].bitcast(FP8X4), zv_s[u // 2][:, cols(u % 2)], zp_q[c][:].bitcast(FP8X4), zp_s[c][:])
+                mx(acc[:, cols(u)], zv_q[u // 2][:, cols(u % 2)].bitcast(FP8X4), zv_s[u // 2][:, cols(u % 2)],
+                   zp_q[c][:].bitcast(FP8X4), zp_s[c][:])
             sums.append(acc)
 
-        def finish(c):
-            pieces = 2 if c == CHUNKS - 1 else 1
-            width = C // pieces
-            for k in range(pieces):
-                part = slice(k * width, (k + 1) * width)
-                nc.vector.tensor_tensor(out=y[c][:, :, part], in0=sums[c][:].rearrange("p (u n) -> p u n", u=PACK)[:, :, part],
-                                        in1=res_t[:, :, cols(c)][:, :, part], op=ALU.add)
-                first = (c % 2) * W + PACK * k * width
-                rounded = y_bf[c // 2][:, first : first + PACK * width]
-                if k == 0:
-                    nc.scalar.copy(out=woven(rounded), in_=planes_walk(y[c][:, :, part]))
-                else:
-                    late.append((rounded, y[c][:, :, part]))
+        def add_residual(c, part):
+            nc.vector.tensor_tensor(out=y[c][:, :, part], in0=sums[c][:].rearrange("p (u n) -> p u n", u=PACK)[:, :, part],
+                                    in1=res_t[:, :, cols(c)][:, :, part], op=ALU.add)
+
+        def rounded(c, part):
+            first = (c % 2) * W
+            return y_bf[c // 2][:, first + PACK * part.start : first + PACK * part.stop]
+
+        def store_rows(c):
             nc.sync.dma_start(out=out_rows[:, :, cols(c)], in_=y[c][:])
 
-        def hand_on(part, source):
-            nc.vector.quantize_mx(out=y_q[:, part].bitcast(FP8X4), scales=y_s[:, part], in_=source)
+        def finish(c):
+            add_residual(c, cols(0))
+            scalar_weave(rounded(c, cols(0)), y[c][:, :, cols(0)])
+            store_rows(c)
+
+        def store_words(h):
+            nc.sync.dma_start(out=out_words[:, half(h)], in_=y_q[:, half(h)].bitcast(I32))
 
         weigh(0)
-        weigh(3)
+        scalar_weave(zp_bf[3][:], zp_planes[:, :, cols(1)])
         zv_s.append(sb("zv_s1", [P, HALF], U8, tag="inv"))
         quantise(zv_q[1][:], zv_s[1][:], zv_bf[1][:])
-        keep_clock("a2", zv_q[1][:, cols(0)], zv_s[1][:, cols(0)])
+        keep_clock(token_banks[1], zv_q[1][:, cols(0)], zv_s[1][:, cols(0)])
         product(0)
         weigh(1)
-        weigh(2)
+        weave(zp_bf[2][:], zp_planes[:, :, cols(0)])
         product(1)
         finish(0)
         product(2)
         product(3)
-        for c in range(1, CHUNKS):
-            finish(c)
-        hand_on(half(0), y_bf[0][:])
-        nc.sync.dma_start(out=out_words[:, half(0)], in_=y_q[:, half(0)].bitcast(I32))
-        for rounded, source in late:
-            weave(rounded, source)
-        hand_on(cols(2), y_bf[1][:, 0:W])
-        hand_on(cols(3), y_bf[1][:, W : 2 * W])
-        nc.sync.dma_start(out=out_words[:, half(1)], in_=y_q[:, half(1)].bitcast(I32))
+        finish(1)
+        finish(2)
+
+        last = CHUNKS - 1
+        front, back = slice(0, C // 2), slice(C // 2, C)
+        add_residual(last, front)
+        scalar_weave(rounded(last, front), y[last][:, :, front])
+        add_residual(last, back)
+        store_rows(last)
+
+        quantise(y_q[:, half(0)], y_s[:, half(0)], y_bf[0][:])
+        store_words(0)
+        weave(rounded(last, back), y[last][:, :, back])
+        quantise(y_q[:, cols(2)], y_s[:, cols(2)], y_bf[1][:, 0:W])
+        quantise(y_q[:, cols(3)], y_s[:, cols(3)], y_bf[1][:, W : 2 * W])
+        store_words(1)
         for q in range(4):
             queue = nc.scalar if q % 2 else nc.sync
             queue.dma_start(out=out_2[0][4 * q : 4 * q + 4, :].bitcast(I32), in_=y_s[32 * q : 32 * q + 4, :].bitcast(I32))

@@ -234,16 +234,10 @@ def tile_picked_listco_none_po_kernel(
             nc.scalar.activation(out=e[:, t, :], in_=acc[:], func=ACT.Exp, bias=low[t][:], scale=-1.0,
                                  accum_out=total[:, t : t + 1])
 
-        def keep_clock(tag, codes, scales):
-            mx(bank(tag, "unread_" + tag)[:], codes.bitcast(FP8X4), scales, z2_q[:].bitcast(FP8X4), z2_s[:])
-
-        for tag in token_banks[2:]:
-            keep_clock(tag, z_q[:, cols(0)], z_s[:, cols(0)])
         weave(zv_bf[1][:], zv_planes[:, :, half(1)])
         zv_q = [sb("zv_q%d" % h, [P, HALF], U32) for h in range(2)]
         zv_s = [sb("zv_s0", [P, HALF], U8)]
         quantise(zv_q[0][:], zv_s[0][:], zv_bf[0][:])
-        keep_clock(token_banks[0], zv_q[0][:, cols(0)], zv_s[0][:, cols(0)])
         inv = sb("inv", [P, PACK], F32)
         factor = sb("factor", [P, PACK], F32)
         nc.vector.reciprocal(out=inv[:], in_=total[:])
@@ -301,7 +295,6 @@ def tile_picked_listco_none_po_kernel(
         scalar_weave(zp_bf[3][:], zp_planes[:, :, cols(1)])
         zv_s.append(sb("zv_s1", [P, HALF], U8, tag="inv"))
         quantise(zv_q[1][:], zv_s[1][:], zv_bf[1][:])
-        keep_clock(token_banks[1], zv_q[1][:, cols(0)], zv_s[1][:, cols(0)])
         product(0)
         weigh(1)
         weave(zp_bf[2][:], zp_planes[:, :, cols(0)])

@@ -58,8 +58,8 @@ def tile_picked_listco_none_po_kernel(
             return slice(h * HALF, (h + 1) * HALF)
 
         def load_plane(plane, scales):
-            for q in range(4):
-                nc.sync.dma_start(out=plane[32 * q : 32 * q + 4, :].bitcast(I32), in_=scales[0][4 * q : 4 * q + 4, :].bitcast(I32))
+            for r in range(4):
+                nc.sync.dma_start(out=plane[r:P:32, :].bitcast(I32), in_=scales[0][r:BLOCKS:4, :].bitcast(I32))
 
         def mx(out, lhs, lhs_scale, rhs, rhs_scale):
             nc.tensor.matmul_mx(out=out, lhsT=lhs, lhsT_scale=lhs_scale, rhs=rhs, rhs_scale=rhs_scale, start=True, stop=True)
@@ -89,7 +89,8 @@ def tile_picked_listco_none_po_kernel(
         w1s = sb("w1s", [P, H], U8)
         rows = [sb("rows%d" % n, [P, P], F32) for n in range(2)]
         ident = sb("ident", [P, P], F32)
-        nc.gpsimd.memset(xs[:].bitcast(I32), 0)
+        nc.gpsimd.memset(xs[:, 0 : T // 2].bitcast(I32), 0)
+        nc.vector.memset(xs[:, T // 2 : T].bitcast(I32), 0)
         nc.vector.memset(rows[0][:], 0.0)
         nc.vector.memset(w2s[:].bitcast(I32), 0)
         nc.vector.memset(w1s[:].bitcast(I32), 0)
@@ -106,11 +107,11 @@ def tile_picked_listco_none_po_kernel(
         res_t = sb("res_t", [P, PACK, V], F32)
         nc.sync.dma_start(qs_t[:], qs)
         nc.sync.dma_start(offs_t[:], offs)
+        nc.sync.dma_start(out=w2w[:].bitcast(I32), in_=w2_words[0].bitcast(I32))
         load_plane(xs, x_scales)
-        load_rows(0, 0, gq)
         nc.scalar.activation(out=rows[1][:], in_=ident[:], func=ACT.Exp)
         nc.sync.dma_start(out=xw[:].bitcast(I32), in_=x_words[0].rearrange("p n t -> p (n t)").bitcast(I32))
-        nc.sync.dma_start(out=w2w[:].bitcast(I32), in_=w2_words[0].bitcast(I32))
+        load_rows(0, 0, gq)
         load_rows(0, 1, gk)
         load_plane(w2s, w2_scales)
         nc.sync.dma_start(out=wv_raw[0][:], in_=wv_rows[:, :, half(0)])

@@ -239,6 +239,8 @@ def tile_picked_listco_none_po_kernel(
         zv_q = [sb("zv_q%d" % h, [P, HALF], U32) for h in range(2)]
         zv_s = [sb("zv_s0", [P, HALF], U8)]
         quantise(zv_q[0][:], zv_s[0][:], zv_bf[0][:])
+        for tag in token_banks[:2]:
+            mx(bank(tag, "unread_" + tag)[:], zv_q[0][:, cols(0)].bitcast(FP8X4), zv_s[0][:, cols(0)], z2_q[:].bitcast(FP8X4), z2_s[:])
         inv = sb("inv", [P, PACK], F32)
         factor = sb("factor", [P, PACK], F32)
         nc.vector.reciprocal(out=inv[:], in_=total[:])

@@ -153,8 +153,9 @@ def tile_picked_listco_none_po_kernel(
         deal(nc.vector, ob, ob_list)
 
         wv_bf = at(0, "wv_bf", [P, PACK * N], BF16)
+        wv_groups = wv_bf[:].rearrange("p (u m t) -> p m t u", u=PACK, t=PACK)
         for h in range(2):
-            scalar_weave(wv_bf[:, 2 * W * h : 2 * W * (h + 1)], wv_raw[h][:])
+            nc.scalar.copy(out=wv_groups[:, h * C // 2 : (h + 1) * C // 2], in_=wv_raw[h][:].rearrange("p t (m u) -> p m t u", u=PACK))
 
         gq_spread = gains[:, 0:PACK].rearrange("p (o t) -> p o t", o=1).to_broadcast([P, C, PACK])
         gk_spread = gains[:, PACK : 2 * PACK].rearrange("p (o t) -> p o t", o=1).to_broadcast([P, C, PACK])
@@ -186,7 +187,7 @@ def tile_picked_listco_none_po_kernel(
         z2_s = sb("z2_s", [P, V], U8)
         quantise(z2_q[:], z2_s[:], z2_bf[:])
 
-        zv_planes = sb("zv_planes", [P, PACK, N], BF16)
+        zv_planes = sb("zv_planes", [P, PACK, W - C], BF16)
         z_planes = sb("z_planes", [P, PACK, W - C], BF16)
         for t in range(PACK):
             acc = bank(("b0", "b1", "b3", "a0")[t], "kf_hi%d" % t)
@@ -205,10 +206,13 @@ def tile_picked_listco_none_po_kernel(
         token_banks = ("b2", "a2", "a3", "b0")
         for t in range(PACK):
             acc = bank(token_banks[t], "val%d" % t)
-            mx(acc[:], ow[:, cols(t)].bitcast(FP8X4), ob[:, cols(t)], wv_q[:].bitcast(FP8X4), wv_s[:])
-            nc.scalar.activation(out=zv_planes[:, t, :].rearrange("p (u m) -> p u m", u=PACK),
-                                 in_=acc[:].rearrange("p (m u) -> p u m", u=PACK),
-                                 func=ACT.Copy, scale=token_gains[:, t : t + 1])
+            for part in (half(0), cols(2)):
+                mx(acc[:, part], ow[:, cols(t)].bitcast(FP8X4), ob[:, cols(t)], wv_q[:, part].bitcast(FP8X4), wv_s[:, part])
+            nc.scalar.activation(out=zv_planes[:, t, :], in_=acc[:, 0 : W - C], func=ACT.Copy, scale=token_gains[:, t : t + 1])
+        val_last = bank("a1", "val_last")
+        for t in range(PACK):
+            mx(val_last[:, cols(t)], ow[:, cols(t)].bitcast(FP8X4), ob[:, cols(t)],
+               wv_q[:, cols(3)].bitcast(FP8X4), wv_s[:, cols(3)])
 
         z_q = sb("z_q", [P, S], U32)
         z_s = sb("z_s", [P, S], U8)
@@ -223,9 +227,10 @@ def tile_picked_listco_none_po_kernel(
         quantise(z_q[:, cols(1)], z_s[:, cols(1)], z_lo[1][:])
         quantise(z_q[:, half(1)], z_s[:, half(1)], z_hi[:])
 
-        zv_bf = [at(4, "zv_lo", [P, 2 * W], BF16), at(2, "zv_hi", [P, 2 * W], BF16)]
-        nc.gpsimd.tensor_scalar(out=zv_bf[0][:].rearrange("p (m t) -> p m t", t=PACK),
-                                in0=zv_planes[:, :, half(0)].rearrange("p t m -> p m t"),
+        zv_all = at(3, "zv_all", [P, PACK * N], BF16)
+        zv_bf = [zv_all[:, 2 * W * h : 2 * W * (h + 1)] for h in range(2)]
+        nc.gpsimd.tensor_scalar(out=zv_all[:, 0 : 3 * W].rearrange("p (m t) -> p m t", t=PACK),
+                                in0=zv_planes[:].rearrange("p t m -> p m t"),
                                 scalar1=1.0, scalar2=0.0, op0=ALU.mult, op1=ALU.add)
 
         for t in range(PACK):
@@ -235,10 +240,11 @@ def tile_picked_listco_none_po_kernel(
             nc.scalar.activation(out=e[:, t, :], in_=acc[:], func=ACT.Exp, bias=low[t][:], scale=-1.0,
                                  accum_out=total[:, t : t + 1])
 
-        weave(zv_bf[1][:], zv_planes[:, :, half(1)])
+        gi_spread = token_gains[:, 0:PACK].rearrange("p (o t) -> p o t", o=1).to_broadcast([P, C, PACK])
+        weigh_woven(zv_all[:, 3 * W : 4 * W], val_last, gi_spread)
         zv_q = [sb("zv_q%d" % h, [P, HALF], U32) for h in range(2)]
         zv_s = [sb("zv_s0", [P, HALF], U8)]
-        quantise(zv_q[0][:], zv_s[0][:], zv_bf[0][:])
+        quantise(zv_q[0][:], zv_s[0][:], zv_bf[0])
         for tag in token_banks[:2]:
             mx(bank(tag, "unread_" + tag)[:], zv_q[0][:, cols(0)].bitcast(FP8X4), zv_s[0][:, cols(0)], z2_q[:].bitcast(FP8X4), z2_s[:])
         inv = sb("inv", [P, PACK], F32)
@@ -297,7 +303,7 @@ def tile_picked_listco_none_po_kernel(
         weigh(0)
         scalar_weave(zp_bf[3][:], zp_planes[:, :, cols(1)])
         zv_s.append(sb("zv_s1", [P, HALF], U8, tag="inv"))
-        quantise(zv_q[1][:], zv_s[1][:], zv_bf[1][:])
+        quantise(zv_q[1][:], zv_s[1][:], zv_bf[1])
         product(0)
         weigh(1)
         weave(zp_bf[2][:], zp_planes[:, :, cols(0)])

@@ -89,12 +89,12 @@ def tile_picked_listco_none_po_kernel(
         w1s = sb("w1s", [P, H], U8)
         rows = [sb("rows%d" % n, [P, P], F32) for n in range(2)]
         ident = sb("ident", [P, P], F32)
-        nc.gpsimd.memset(xs[:, 0 : T // 2].bitcast(I32), 0)
-        nc.vector.memset(xs[:, T // 2 : T].bitcast(I32), 0)
+        nc.vector.memset(xs[:].bitcast(I32), 0)
         nc.vector.memset(rows[0][:], 0.0)
+        nc.vector.memset(ident[:], 0.0)
         nc.vector.memset(w2s[:].bitcast(I32), 0)
         nc.vector.memset(w1s[:].bitcast(I32), 0)
-        make_identity(nc, ident[:])
+        make_identity(nc, ident[:], nomemset=True)
 
         def load_rows(n, m, vec):
             nc.sync.dma_start(

@@ -137,20 +137,20 @@ def tile_picked_listco_none_po_kernel(
         w2sd = sb("w2sd", [P, H], U8)
         w1sd = sb("w1sd", [P, H], U8)
 
-        def deal(engine, dealt, plain):
-            engine.tensor_copy(
-                out=dealt[:].bitcast(I32).rearrange("p (t b q) -> p t b q", t=PACK, b=BLOCKS),
-                in_=plain[:].bitcast(I32).rearrange("p (b t q) -> p t b q", t=PACK, b=BLOCKS),
+        def deal(copy, dealt, plain):
+            copy(
+                out=dealt[:].bitcast(U32).rearrange("p (t b q) -> p t b q", t=PACK, b=BLOCKS),
+                in_=plain[:].bitcast(U32).rearrange("p (b t q) -> p t b q", t=PACK, b=BLOCKS),
             )
 
         nc.vector.tensor_copy(qb[:], xs[:].indirect(qs_t[:]))
         nc.vector.tensor_copy(ob_list[:], xs[:].indirect(offs_t[:]))
         nc.vector.tensor_copy(qw[:], xw[:].indirect(qs_t[:]))
-        deal(nc.gpsimd, w2wd, w2w)
-        deal(nc.gpsimd, w2sd, w2s)
+        deal(nc.scalar.copy, w2wd, w2w)
+        deal(nc.scalar.copy, w2sd, w2s)
         ow = sb("ow", [P, S], U32)
         nc.vector.tensor_copy(ow[:].rearrange("p (t b r) -> p b t r", t=PACK, b=BLOCKS), xw[:].indirect(offs_t[:]))
-        deal(nc.vector, ob, ob_list)
+        deal(nc.vector.tensor_copy, ob, ob_list)
 
         wv_bf = at(0, "wv_bf", [P, PACK * N], BF16)
         wv_groups = wv_bf[:].rearrange("p (u m t) -> p m t u", u=PACK, t=PACK)
@@ -178,8 +178,8 @@ def tile_picked_listco_none_po_kernel(
         for c in range(CHUNKS):
             weigh_woven(z2_bf[:, c * W : (c + 1) * W], chunk_product("a%d" % c, "qf%d" % c, w2wd, w2sd, qw, qb, c), gq_spread)
 
-        deal(nc.gpsimd, w1wd, w1w)
-        deal(nc.gpsimd, w1sd, w1s)
+        deal(nc.gpsimd.tensor_copy, w1wd, w1w)
+        deal(nc.gpsimd.tensor_copy, w1sd, w1s)
         wv_q = sb("wv_q", [P, N], U32)
         wv_s = sb("wv_s", [P, N], U8, tag="w1s")
         quantise(wv_q[:], wv_s[:], wv_bf[:])

from contextlib import ExitStack

import concourse.mybir as mybir
from concourse.masks import make_identity

T, S, V, N, H = 2048, 512, 512, 512, 512
FLOPS = 5 * 2 * 512 * 512 * 512

F32 = mybir.dt.float32
BF16 = mybir.dt.bfloat16
I32 = mybir.dt.int32
U32 = mybir.dt.uint32
U16 = mybir.dt.uint16
U8 = mybir.dt.uint8
FP8X4 = mybir.dt.float8_e4m3fn_x4
FP4X4 = mybir.dt.float4_e2m1fn_x4
ACT = mybir.ActivationFunctionType
ALU = mybir.AluOpType

P = 128
PACK = 4
BLOCKS = 16
RUN = 8
W = 512
C = 128
HALF = 256
CHUNKS = W // C
WALK = 4
KIB = 1024
SHARED = 0


def tile_picked_listco_none_po_kernel(
    tc, x_words, x_scales, w1_words, w1_scales, w2_words, w2_scales, gk, gq, wv, gi, res, gt, offs, qs,
    out_0, out_1, out_2,
):
    nc = tc.nc

    with ExitStack() as ctx:
        lists = ctx.enter_context(tc.tile_pool(name="lists", bufs=1))
        keep = ctx.enter_context(tc.tile_pool(name="keep", bufs=1))
        placed = ctx.enter_context(tc.tile_pool(name="placed", bufs=1))
        psum = ctx.enter_context(tc.psum_pool(name="psum", bufs=1))

        def sb(name, shape, dtype, tag=None):
            return keep.tile(shape, dtype, name=name, tag=tag or name, align_bytes=64)

        def at(kib, name, shape, dtype):
            return placed.tile(shape, dtype, name=name, align_bytes=64, offset=SHARED + kib * KIB)

        def bank(tag, name):
            return psum.tile([P, W], F32, name=name, tag=tag)

        def cols(c):
            return slice(c * C, (c + 1) * C)

        def half(h):
            return slice(h * HALF, (h + 1) * HALF)

        def load_plane(plane, scales):
            for r in range(4):
                nc.sync.dma_start(out=plane[r:P:32, :].bitcast(I32), in_=scales[0][r:BLOCKS:4, :].bitcast(I32))

        def mx(out, lhs, lhs_scale, rhs, rhs_scale):
            nc.tensor.matmul_mx(out=out, lhsT=lhs, lhsT_scale=lhs_scale, rhs=rhs, rhs_scale=rhs_scale, start=True, stop=True)

        def quantise(codes, scales, source):
            nc.vector.quantize_mx(out=codes.bitcast(FP8X4), scales=scales, in_=source)

        def woven(tile_ap):
            return tile_ap.rearrange("p (c i t) -> p c t i", i=WALK, t=PACK)

        def planes_walk(planes_ap):
            return planes_ap.rearrange("p t (c i) -> p c t i", i=WALK)

        def weave(dst, planes_ap):
            nc.vector.tensor_copy(out=woven(dst), in_=planes_walk(planes_ap))

        def scalar_weave(dst, planes_ap):
            nc.scalar.copy(out=woven(dst), in_=planes_walk(planes_ap))

        qs_t = lists.tile([P, V // 16], U16, name="qs_t")
        offs_t = lists.tile([P, S // 16], U16, name="offs_t")
        xs = sb("xs", [P, T], U8)
        xw = sb("xw", [P, T], U32)
        w2w = sb("w2w", [P, 2 * H], U8)
        w2s = sb("w2s", [P, H], U8)
        w1w = sb("w1w", [P, 2 * H], U8)
        w1s = sb("w1s", [P, H], U8)
        rows = [sb("rows%d" % n, [P, P], F32) for n in range(2)]
        ident = sb("ident", [P, P], F32)
        nc.vector.memset(xs[:].bitcast(I32), 0)
        nc.vector.memset(rows[0][:], 0.0)
        nc.vector.memset(ident[:], 0.0)
        nc.vector.memset(w2s[:].bitcast(I32), 0)
        nc.vector.memset(w1s[:].bitcast(I32), 0)
        make_identity(nc, ident[:], nomemset=True)

        def load_rows(n, m, vec):
            nc.sync.dma_start(
                out=rows[n][PACK * m : PACK * (m + 1), :].rearrange("t (b r) -> t b r", r=RUN),
                in_=vec.rearrange("(b t r) o -> t b (r o)", t=PACK, r=RUN),
            )

        wv_raw = [sb("wv_raw%d" % h, [P, PACK, HALF], F32) for h in range(2)]
        wv_rows = wv.rearrange("(p j) n -> p j n", j=PACK)
        res_t = sb("res_t", [P, PACK, V], F32)
        nc.sync.dma_start(qs_t[:], qs)
        nc.sync.dma_start(offs_t[:], offs)
        nc.sync.dma_start(out=w2w[:].bitcast(I32), in_=w2_words[0].bitcast(I32))
        load_plane(xs, x_scales)
        nc.scalar.activation(out=rows[1][:], in_=ident[:], func=ACT.Exp)
        nc.sync.dma_start(out=xw[:].bitcast(I32), in_=x_words[0].rearrange("p n t -> p (n t)").bitcast(I32))
        load_rows(0, 0, gq)
        load_rows(0, 1, gk)
        load_plane(w2s, w2_scales)
        nc.sync.dma_start(out=wv_raw[0][:], in_=wv_rows[:, :, half(0)])
        nc.sync.dma_start(out=wv_raw[1][:], in_=wv_rows[:, :, half(1)])
        nc.sync.dma_start(out=w1w[:].bitcast(I32), in_=w1_words[0].bitcast(I32))
        load_rows(1, 0, gi)
        load_rows(1, 1, gt)
        load_plane(w1s, w1_scales)
        nc.sync.dma_start(out=res_t[:], in_=res.rearrange("(p t) v -> p t v", t=PACK))

        turned = bank("b3", "turned")
        nc.tensor.transpose(turned[:, 0:P], rows[0][:], ident[:])
        gains = sb("gains", [P, 2 * PACK], F32)
        nc.scalar.activation(out=gains[:, 0:PACK], in_=turned[:, 0:PACK], func=ACT.Copy, scale=-0.03125)
        nc.scalar.copy(out=gains[:, PACK : 2 * PACK], in_=turned[:, PACK : 2 * PACK])

        qb = sb("qb", [P, V], U8)
        qw = sb("qw", [P, V], U32)
        ob_list = sb("ob_list", [P, S], U8)
        ob = sb("ob", [P, S], U8, tag="w2s")
        w2wd = sb("w2wd", [P, 2 * H], U8)
        w1wd = sb("w1wd", [P, 2 * H], U8)
        w2sd = sb("w2sd", [P, H], U8)
        w1sd = sb("w1sd", [P, H], U8)

        def deal(copy, dealt, plain):
            copy(
                out=dealt[:].bitcast(U32).rearrange("p (t b q) -> p t b q", t=PACK, b=BLOCKS),
                in_=plain[:].bitcast(U32).rearrange("p (b t q) -> p t b q", t=PACK, b=BLOCKS),
            )

        nc.vector.tensor_copy(qb[:], xs[:].indirect(qs_t[:]))
        nc.vector.tensor_copy(ob_list[:], xs[:].indirect(offs_t[:]))
        nc.vector.tensor_copy(qw[:], xw[:].indirect(qs_t[:]))
        deal(nc.scalar.copy, w2wd, w2w)
        deal(nc.scalar.copy, w2sd, w2s)
        ow = sb("ow", [P, S], U32)
        nc.vector.tensor_copy(ow[:].rearrange("p (t b r) -> p b t r", t=PACK, b=BLOCKS), xw[:].indirect(offs_t[:]))
        deal(nc.vector.tensor_copy, ob, ob_list)

        wv_bf = at(0, "wv_bf", [P, PACK * N], BF16)
        wv_groups = wv_bf[:].rearrange("p (u m t) -> p m t u", u=PACK, t=PACK)
        for h in range(2):
            nc.scalar.copy(out=wv_groups[:, h * C // 2 : (h + 1) * C // 2], in_=wv_raw[h][:].rearrange("p t (m u) -> p m t u", u=PACK))

        gq_spread = gains[:, 0:PACK].rearrange("p (o t) -> p o t", o=1).to_broadcast([P, C, PACK])
        gk_spread = gains[:, PACK : 2 * PACK].rearrange("p (o t) -> p o t", o=1).to_broadcast([P, C, PACK])

        def fp4_slot(words, t):
            return words[:, 2 * C * t : 2 * C * (t + 1)].bitcast(FP4X4)

        def chunk_product(tag, name, words, plane, picked_words, picked_plane, c):
            acc = bank(tag, name)
            for t in range(PACK):
                mx(acc[:, cols(t)], fp4_slot(words, t), plane[:, cols(t)],
                   picked_words[:, cols(c)].bitcast(FP8X4), picked_plane[:, cols(c)])
            return acc

        def weigh_woven(dst, acc, spread):
            nc.vector.tensor_tensor(out=dst.rearrange("p (n t) -> p n t", t=PACK),
                                    in0=acc[:].rearrange("p (t n) -> p n t", t=PACK), in1=spread, op=ALU.mult)

        z2_bf = sb("z2_bf", [P, PACK * V], BF16)
        for c in range(CHUNKS):
            weigh_woven(z2_bf[:, c * W : (c + 1) * W], chunk_product("a%d" % c, "qf%d" % c, w2wd, w2sd, qw, qb, c), gq_spread)

        deal(nc.gpsimd.tensor_copy, w1wd, w1w)
        deal(nc.gpsimd.tensor_copy, w1sd, w1s)
        wv_q = sb("wv_q", [P, N], U32)
        wv_s = sb("wv_s", [P, N], U8, tag="w1s")
        quantise(wv_q[:], wv_s[:], wv_bf[:])
        z2_q = at(0, "z2_q", [P, V], U32)
        z2_s = sb("z2_s", [P, V], U8)
        quantise(z2_q[:], z2_s[:], z2_bf[:])

        zv_planes = sb("zv_planes", [P, PACK, W - C], BF16)
        z_planes = sb("z_planes", [P, PACK, W - C], BF16)
        for t in range(PACK):
            acc = bank(("b0", "b1", "b3", "a0")[t], "kf_hi%d" % t)
            for part in (cols(1), half(1)):
                mx(acc[:, part], fp4_slot(w1wd, t), w1sd[:, cols(t)], ow[:, part].bitcast(FP8X4), ob[:, part])
            nc.scalar.activation(out=z_planes[:, t, :], in_=acc[:, C:W], func=ACT.Copy, scale=gains[:, PACK + t : PACK + t + 1])

        z_lo = [sb("z_lo0", [P, W], BF16), at(2, "z_lo1", [P, W], BF16)]
        weigh_woven(z_lo[0][:], chunk_product("a1", "kf0", w1wd, w1sd, ow, ob, 0), gk_spread)

        turned2 = bank("b2", "turned2")
        nc.tensor.transpose(turned2[:, 0:P], rows[1][:], ident[:])
        token_gains = sb("token_gains", [P, 2 * PACK], F32)
        nc.scalar.copy(out=token_gains[:], in_=turned2[:, 0 : 2 * PACK])

        token_banks = ("b2", "a2", "a3", "b0")
        for t in range(PACK):
            acc = bank(token_banks[t], "val%d" % t)
            for part in (half(0), cols(2)):
                mx(acc[:, part], ow[:, cols(t)].bitcast(FP8X4), ob[:, cols(t)], wv_q[:, part].bitcast(FP8X4), wv_s[:, part])
            nc.scalar.activation(out=zv_planes[:, t, :], in_=acc[:, 0 : W - C], func=ACT.Copy, scale=token_gains[:, t : t + 1])
        val_last = bank("a1", "val_last")
        for t in range(PACK):
            mx(val_last[:, cols(t)], ow[:, cols(t)].bitcast(FP8X4), ob[:, cols(t)],
               wv_q[:, cols(3)].bitcast(FP8X4), wv_s[:, cols(3)])

        z_q = sb("z_q", [P, S], U32)
        z_s = sb("z_s", [P, S], U8)
        low = [sb("low%d" % t, [P, 1], F32) for t in range(PACK)]
        total = sb("total", [P, PACK], F32)
        e = sb("e", [P, PACK, V], F32)

        weave(z_lo[1][:], z_planes[:, :, cols(0)])
        quantise(z_q[:, cols(0)], z_s[:, cols(0)], z_lo[0][:])
        z_hi = at(3, "z_hi", [P, 2 * W], BF16)
        weave(z_hi[:], z_planes[:, :, C : W - C])
        quantise(z_q[:, cols(1)], z_s[:, cols(1)], z_lo[1][:])
        quantise(z_q[:, half(1)], z_s[:, half(1)], z_hi[:])

        zv_all = at(3, "zv_all", [P, PACK * N], BF16)
        zv_bf = [zv_all[:, 2 * W * h : 2 * W * (h + 1)] for h in range(2)]
        nc.gpsimd.tensor_scalar(out=zv_all[:, 0 : 3 * W].rearrange("p (m t) -> p m t", t=PACK),
                                in0=zv_planes[:].rearrange("p t m -> p m t"),
                                scalar1=1.0, scalar2=0.0, op0=ALU.mult, op1=ALU.add)

        for t in range(PACK):
            acc = bank(token_banks[t], "s%d" % t)
            mx(acc[:], z_q[:, cols(t)].bitcast(FP8X4), z_s[:, cols(t)], z2_q[:].bitcast(FP8X4), z2_s[:])
            nc.vector.tensor_reduce(out=low[t][:], in_=acc[:], axis=mybir.AxisListType.X, op=ALU.min)
            nc.scalar.activation(out=e[:, t, :], in_=acc[:], func=ACT.Exp, bias=low[t][:], scale=-1.0,
                                 accum_out=total[:, t : t + 1])

        gi_spread = token_gains[:, 0:PACK].rearrange("p (o t) -> p o t", o=1).to_broadcast([P, C, PACK])
        weigh_woven(zv_all[:, 3 * W : 4 * W], val_last, gi_spread)
        zv_q = [sb("zv_q%d" % h, [P, HALF], U32) for h in range(2)]
        zv_s = [sb("zv_s0", [P, HALF], U8)]
        quantise(zv_q[0][:], zv_s[0][:], zv_bf[0])
        for tag in token_banks[:2]:
            mx(bank(tag, "unread_" + tag)[:], zv_q[0][:, cols(0)].bitcast(FP8X4), zv_s[0][:, cols(0)], z2_q[:].bitcast(FP8X4), z2_s[:])
        inv = sb("inv", [P, PACK], F32)
        factor = sb("factor", [P, PACK], F32)
        nc.vector.reciprocal(out=inv[:], in_=total[:])
        nc.vector.scalar_tensor_tensor(out=factor[:], in0=inv[:], scalar=16.0, in1=token_gains[:, PACK : 2 * PACK],
                                       op0=ALU.mult, op1=ALU.mult)
        factor_spread = factor[:].rearrange("p (a t b) -> p a t b", a=1, b=1).to_broadcast([P, C // WALK, PACK, WALK])

        zp_bf = [sb("zp_bf%d" % c, [P, W], BF16) for c in range(CHUNKS)]
        zp_q = [sb("zp_q%d" % c, [P, C], U32) for c in range(CHUNKS)]
        zp_s = [sb("zp_s%d" % c, [P, C], U8) for c in range(CHUNKS)]
        y = [sb("y%d" % c, [P, PACK, C], F32) for c in range(CHUNKS)]
        y_bf = [sb("y_bf%d" % h, [P, 2 * W], BF16) for h in range(2)]
        y_q = sb("y_q", [P, V], U32)
        y_s = sb("y_s", [P, V], U8)
        out_rows = out_0.rearrange("(p t) v -> p t v", t=PACK)
        out_words = out_1[0].rearrange("p n t -> p (n t)").bitcast(I32)
        result_banks = ("b1", "b3", "a0", "a1")
        sums = []

        zp_planes = sb("zp_planes", [P, PACK, HALF], BF16)
        for t in range(PACK):
            nc.scalar.activation(out=zp_planes[:, t, :], in_=e[:, t, half(1)], func=ACT.Copy, scale=factor[:, t : t + 1])

        def weigh(c):
            nc.vector.tensor_tensor(out=woven(zp_bf[c][:]), in0=planes_walk(e[:, :, cols(c)]), in1=factor_spread, op=ALU.mult)

        def product(c):
            quantise(zp_q[c][:], zp_s[c][:], zp_bf[c][:])
            acc = bank(result_banks[c], "y_acc%d" % c)
            for u in range(PACK):
                mx(acc[:, cols(u)], zv_q[u // 2][:, cols(u % 2)].bitcast(FP8X4), zv_s[u // 2][:, cols(u % 2)],
                   zp_q[c][:].bitcast(FP8X4), zp_s[c][:])
            sums.append(acc)

        def add_residual(c, part):
            nc.vector.tensor_tensor(out=y[c][:, :, part], in0=sums[c][:].rearrange("p (u n) -> p u n", u=PACK)[:, :, part],
                                    in1=res_t[:, :, cols(c)][:, :, part], op=ALU.add)

        def rounded(c, part):
            first = (c % 2) * W
            return y_bf[c // 2][:, first + PACK * part.start : first + PACK * part.stop]

        def store_rows(c):
            nc.sync.dma_start(out=out_rows[:, :, cols(c)], in_=y[c][:])

        def finish(c):
            add_residual(c, cols(0))
            scalar_weave(rounded(c, cols(0)), y[c][:, :, cols(0)])
            store_rows(c)

        def store_words(h):
            nc.sync.dma_start(out=out_words[:, half(h)], in_=y_q[:, half(h)].bitcast(I32))

        weigh(0)
        scalar_weave(zp_bf[3][:], zp_planes[:, :, cols(1)])
        zv_s.append(sb("zv_s1", [P, HALF], U8, tag="inv"))
        quantise(zv_q[1][:], zv_s[1][:], zv_bf[1])
        product(0)
        weigh(1)
        weave(zp_bf[2][:], zp_planes[:, :, cols(0)])
        product(1)
        finish(0)
        product(2)
        product(3)
        finish(1)
        finish(2)

        last = CHUNKS - 1
        front, back = slice(0, C // 2), slice(C // 2, C)
        add_residual(last, front)
        scalar_weave(rounded(last, front), y[last][:, :, front])
        add_residual(last, back)
        store_rows(last)

        quantise(y_q[:, half(0)], y_s[:, half(0)], y_bf[0][:])
        store_words(0)
        weave(rounded(last, back), y[last][:, :, back])
        quantise(y_q[:, cols(2)], y_s[:, cols(2)], y_bf[1][:, 0:W])
        quantise(y_q[:, cols(3)], y_s[:, cols(3)], y_bf[1][:, W : 2 * W])
        store_words(1)
        for q in range(4):
            queue = nc.scalar if q % 2 else nc.sync
            queue.dma_start(out=out_2[0][4 * q : 4 * q + 4, :].bitcast(I32), in_=y_s[32 * q : 32 * q + 4, :].bitcast(I32))
